import numpy as np
import ml_dtypes


def mxq(x, axis, fmt="e4m3"):
    dtype, down = {"e4m3": (ml_dtypes.float8_e4m3fn, 7), "e5m2": (ml_dtypes.float8_e5m2, 14)}[fmt]
    v = np.moveaxis(np.asarray(x, np.float32).astype(ml_dtypes.bfloat16).astype(np.float64), axis, -1)
    blocks = v.reshape(v.shape[:-1] + (-1, 32))
    amax = np.abs(blocks).max(-1, keepdims=True)
    byte = np.maximum(np.where(amax > 0, np.frexp(amax)[1] - 1 + 127, 0) - down, 1)
    scale = np.exp2(byte - 127.0)
    codes = (blocks / scale).astype(np.float32).astype(dtype).astype(np.float64)
    return np.moveaxis((codes * scale).reshape(v.shape), -1, axis)


WIDE = False


def mx_kscale(k):
    if not WIDE:
        return np.ones(k)
    levels = np.array([18, -18])
    if k % 512:
        return np.exp2(np.random.permutation(np.resize(levels, k // 32))).repeat(32)
    a = np.empty((k // 512, 16))
    for p in range(k // 512):
        a[p, :8] = np.random.permutation(np.resize(levels, 8))
        for g in range(8):
            far = levels[np.abs(levels - a[p, g]) >= 10]
            a[p, g + 8] = far[np.random.randint(len(far))]
    return np.exp2(a.ravel()).repeat(32)


def f64(x):
    return np.asarray(x).astype(np.float64)


def striped(idx):
    return np.tile(np.asarray(idx).reshape(-1, 16).T, (8, 1)).astype(np.uint16)


def unstriped(offs):
    return offs[:16].T.reshape(-1).astype(np.int64)


B, N, T, D, R, TU = 2, 512, 2048, 512, 512, 2048


def setup_inputs():
    n = np.random.standard_normal
    idx = np.random.permutation(T)[:B * N]
    uidx = np.random.permutation(TU)[:B * R]
    s = mx_kscale(D)[:, None]
    z = np.ones(TU)
    z[uidx] = mx_kscale(B * R)
    u = np.ones(T)
    u[idx] = mx_kscale(B * N)
    r = np.random.uniform(0.5, 2.0, T) * u
    ur = np.random.uniform(0.5, 2.0, TU) * z
    return {
        "uT": (n((D, TU)) * s / ur).astype(np.float32),
        "vT": (n((D, T)) * (1.00 / np.sqrt(D)) / s / r).astype(np.float32),
        "y": np.random.randint(0, 2, (B, R, N)).astype(np.float32),
        "us": ur[uidx].reshape(B, R, 1).astype(np.float32),
        "ts": np.tile(r, (128, 1)).astype(np.float32),
        "offs": striped(idx),
        "uoffs": striped(uidx),
    }


def reference(uT, vT, y, us, ts, offs, uoffs):
    idx = unstriped(offs)
    pick = lambda x: x[:, idx].reshape(x.shape[0], B, N).transpose(1, 0, 2)
    uidx = unstriped(uoffs)
    w = pick(f64(vT))
    x = f64(uT)[:, uidx].reshape(D, B, R).transpose(1, 0, 2)
    a = mxq(x, 1, "e4m3").transpose(0, 2, 1) @ mxq(w, 1, "e4m3")
    sc = f64(us) * pick(f64(ts))[:, :1, :]
    a = a * sc
    g = (1.0 / (1.0 + np.exp(-a)) - f64(y))
    h = sc * g
    dv = mxq(x, 2, "e4m3") @ mxq(h, 1, "e5m2")
    gv = np.zeros((D, T))
    gv[:, idx] = dv.transpose(1, 0, 2).reshape(D, B * N)
    du = mxq(w, 2, "e4m3") @ mxq(h, 2, "e5m2").transpose(0, 2, 1)
    gu = np.zeros((D, TU))
    gu[:, uidx] = du.transpose(1, 0, 2).reshape(D, B * R)
    return gv, gu

@@ -1,0 +1,241 @@
+from contextlib import ExitStack
+
+import concourse.mybir as mybir
+from concourse.masks import make_identity
+
+B, N, T, D, R, TU = 2, 512, 2048, 512, 512, 2048
+FLOPS = 3 * 2 * B * R * N * D
+
+F32 = mybir.dt.float32
+BF16 = mybir.dt.bfloat16
+U32 = mybir.dt.uint32
+U16 = mybir.dt.uint16
+U8 = mybir.dt.uint8
+E4M3 = mybir.dt.float8_e4m3fn_x4
+E5M2 = mybir.dt.float8_e5m2_x4
+MULT = mybir.AluOpType.mult
+SUBTRACT = mybir.AluOpType.subtract
+COPY = mybir.ActivationFunctionType.Copy
+SIGMOID = mybir.ActivationFunctionType.Sigmoid
+
+P = 128
+PACK = 4
+K = P * PACK
+LIST_COLS = K // 16
+
+
+def tile_attend_gmf_nce_vu_kernel(tc, uT, vT, y, us, ts, offs, uoffs, out_0, out_1):
+    nc = tc.nc
+    with ExitStack() as ctx:
+        keep = ctx.enter_context(tc.tile_pool(name="keep", bufs=1))
+        big = ctx.enter_context(tc.tile_pool(name="big", bufs=7))
+        pairs = ctx.enter_context(tc.tile_pool(name="pairs", bufs=3))
+        packed = ctx.enter_context(tc.tile_pool(name="packed", bufs=4))
+        turned = ctx.enter_context(tc.tile_pool(name="turned", bufs=2))
+        quant = ctx.enter_context(tc.tile_pool(name="quant", bufs=8))
+        staged = ctx.enter_context(tc.tile_pool(name="staged", bufs=8))
+        logit_ps = ctx.enter_context(tc.psum_pool(name="logit_ps", bufs=4))
+        turn_ps = ctx.enter_context(tc.psum_pool(name="turn_ps", bufs=2))
+        grad_ps = ctx.enter_context(tc.psum_pool(name="grad_ps", bufs=2))
+
+        head_list = keep.tile([P, B * LIST_COLS], U16, name="head_list")
+        tail_list = keep.tile([P, B * LIST_COLS], U16, name="tail_list")
+        row_scale = keep.tile([P, B, PACK], F32, name="row_scale")
+        ident = keep.tile([P, P], F32, name="ident")
+        warm = keep.tile([P, 8], F32, name="warm")
+        warm_out = keep.tile([P, 8], F32, name="warm_out")
+        make_identity(nc, ident[:])
+        nc.vector.memset(warm[:], 0.0)
+        nc.scalar.activation(warm_out[:], warm[:], SIGMOID)
+
+        def group(lst, b):
+            return lst[:, b * LIST_COLS : (b + 1) * LIST_COLS]
+
+        def load_pair(table, u, cuts, name):
+            rows = table.rearrange("(p u e) c -> p u e c", u=2, e=2)
+            pair = pairs.tile([P, T, 2], BF16, name=name, tag="pair")
+            for c0, c1, on_vector in cuts:
+                raw = big.tile([P, 2, c1 - c0], F32, name="raw", tag="big")
+                nc.sync.dma_start(raw[:], rows[:, u, :, c0:c1])
+                src = raw[:].rearrange("p e c -> p c e")
+                if on_vector:
+                    nc.vector.tensor_copy(pair[:, c0:c1, :], src)
+                else:
+                    nc.scalar.activation(pair[:, c0:c1, :], src, COPY)
+            return pair
+
+        def gather_pair(dst, u, pair, lst):
+            window = pair[:].rearrange("p c e -> p (c e)").bitcast(U32)
+            nc.vector.tensor_copy(dst[:, u, :].bitcast(U32), window.indirect(lst))
+
+        def quantize(src, fmt):
+            codes = quant.tile([P, K], U32, name="codes", tag="codes", align_bytes=64)
+            scales = quant.tile([P, K], U8, name="scales", tag="scales", align_bytes=64)
+            nc.vector.quantize_mx(codes[:].bitcast(fmt), scales[:], src[:])
+            return codes, scales, fmt
+
+        def mx(dst, stationary, t, moving):
+            cols = slice(t * P, (t + 1) * P)
+            nc.tensor.matmul_mx(
+                dst,
+                lhsT=stationary[0][:, cols].bitcast(stationary[2]),
+                lhsT_scale=stationary[1][:, cols],
+                rhs=moving[0][:].bitcast(moving[2]),
+                rhs_scale=moving[1][:],
+                start=True,
+                stop=True,
+            )
+
+        def turn(words, natural, on_vector):
+            dst = turned.tile([P, K * PACK], BF16, name="turned", tag="turned", align_bytes=64)
+            for u in range(2):
+                bank = turn_ps.tile([P, PACK, P], F32, name="bank", tag="bank")
+                for s in range(PACK):
+                    nc.tensor.transpose(bank[:, s, :], words(u, s), ident[:])
+                halves = bank[:].rearrange("q s p -> q (s p)").bitcast(BF16)
+                if natural:
+                    src = halves.rearrange("q (s p e) -> q p e s", s=PACK, e=2)
+                    out = dst[:].rearrange("q (p u e s) -> q u p e s", u=2, e=2, s=PACK)[:, u]
+                else:
+                    src = halves.rearrange("q (s p e) -> q e p s", s=PACK, e=2)
+                    out = dst[:].rearrange("q (u e p s) -> q u e p s", u=2, e=2, s=PACK)[:, u]
+                if on_vector:
+                    nc.vector.tensor_copy(out, src)
+                else:
+                    nc.scalar.copy(out, src)
+            return dst
+
+        def packed_words(tile):
+            words = tile[:].bitcast(F32).rearrange("p (s q u) -> p u s q", s=PACK, u=2)
+            return lambda u, s: words[:, u, s, :]
+
+        def gathered_words(tile):
+            words = tile[:].rearrange("p u x -> p (u x)").bitcast(F32).rearrange("p (u q s) -> p u s q", u=2, s=PACK)
+            return lambda u, s: words[:, u, s, :]
+
+        halves_cut = [(0, T // 2, False), (T // 2, T, False)]
+        last_cut = [(0, T // 2, False), (T // 2, 3 * T // 4, True), (3 * T // 4, T, True)]
+
+        heads = [keep.tile([P, 2, 2 * K], BF16, name="heads%d" % b) for b in range(B)]
+        tails = [keep.tile([P, 2, 2 * K], BF16, name="tails%d" % b) for b in range(B)]
+
+        u_pair0 = load_pair(uT, 0, halves_cut, "u_pair0")
+        nc.sync.dma_start(head_list[:], uoffs)
+        nc.sync.dma_start(tail_list[:], offs)
+        nc.sync.dma_start(row_scale[:], us.rearrange("b (p t) o -> p b (t o)", t=PACK))
+        u_pair1 = load_pair(uT, 1, halves_cut, "u_pair1")
+        for u, pair in enumerate((u_pair0, u_pair1)):
+            for b in range(B):
+                gather_pair(heads[b], u, pair, group(head_list, b))
+        v_pair0 = load_pair(vT, 0, halves_cut, "v_pair0")
+        v_pair1 = load_pair(vT, 1, last_cut, "v_pair1")
+        tail_scale_all = big.tile([P, T], F32, name="tail_scale_all", tag="big")
+        nc.sync.dma_start(tail_scale_all[:], ts)
+        labels = []
+        for b in range(B):
+            lab = big.tile([P, PACK, N], F32, name="labels", tag="big")
+            nc.sync.dma_start(lab[:], y[b].rearrange("(p t) i -> p t i", t=PACK))
+            labels.append(lab)
+
+        def heads_along_d(b):
+            x = packed.tile([P, K * PACK], BF16, name="x", tag="packed", align_bytes=64)
+            nc.vector.tensor_copy(
+                x[:].rearrange("p (s q u e) -> p q s u e", s=PACK, u=2, e=2),
+                heads[b][:].rearrange("p u (q s e) -> p q s u e", s=PACK, e=2),
+            )
+            return x, quantize(x, E4M3)
+
+        def tails_along_d(b):
+            w = packed.tile([P, K * PACK], BF16, name="w", tag="packed", align_bytes=64)
+            nc.vector.tensor_copy(
+                w[:].rearrange("p (i u e) -> p i u e", u=2, e=2),
+                tails[b][:].rearrange("p u (i e) -> p i u e", e=2),
+            )
+            return quantize(w, E4M3)
+
+        def scale_product(b):
+            picked = keep.tile([P, N], F32, name="picked%d" % b)
+            nc.vector.tensor_copy(picked[:], tail_scale_all[:].indirect(group(tail_list, b)))
+            sc = big.tile([P, PACK, N], F32, name="sc", tag="big")
+            for t in range(PACK):
+                nc.scalar.activation(sc[:, t, :], picked[:], COPY, scale=row_scale[:, b, t : t + 1])
+            return sc
+
+        def weights(b, xq, wq, sc, on_vector):
+            eng = nc.vector if on_vector else nc.gpsimd
+            z = big.tile([P, PACK, N], F32, name="z", tag="big")
+            for t in range(PACK):
+                acc = logit_ps.tile([P, N], F32, name="acc", tag="acc")
+                mx(acc[:], xq, t, wq)
+                if on_vector:
+                    nc.vector.tensor_tensor(z[:, t, :], acc[:], sc[:, t, :], MULT)
+                else:
+                    nc.scalar.copy(z[:, t, :], acc[:])
+                    nc.gpsimd.tensor_tensor(z[:, t, :], z[:, t, :], sc[:, t, :], MULT)
+                nc.scalar.activation(z[:, t, :], z[:, t, :], SIGMOID)
+            for t in range(PACK):
+                eng.tensor_tensor(z[:, t, :], z[:, t, :], labels[b][:, t, :], SUBTRACT)
+            h = packed.tile([P, K * PACK], BF16, name="h", tag="packed", align_bytes=64)
+            eng.tensor_tensor(
+                h[:].rearrange("p (s q t) -> p q s t", s=PACK, t=PACK),
+                z[:].rearrange("p t (q s) -> p q s t", s=PACK),
+                sc[:].rearrange("p t (q s) -> p q s t", s=PACK),
+                MULT,
+            )
+            return h
+
+        def gradient(stationary, moving, permuted):
+            tiles = []
+            for t in range(PACK):
+                acc = grad_ps.tile([P, K], F32, name="grad", tag="grad")
+                mx(acc[:], stationary, t, moving)
+                st = staged.tile([P, K], F32, name="staged", tag="staged")
+                if permuted:
+                    nc.scalar.copy(
+                        st[:].rearrange("p (q s) -> p q s", s=PACK), acc[:].rearrange("p (s q) -> p q s", s=PACK)
+                    )
+                else:
+                    nc.scalar.copy(st[:], acc[:])
+                tiles.append(st)
+            return tiles
+
+        x0, xq0 = heads_along_d(0)
+        for u, pair in enumerate((v_pair0, v_pair1)):
+            gather_pair(tails[0], u, pair, group(tail_list, 0))
+        wq0 = tails_along_d(0)
+        sc0 = scale_product(0)
+        h0 = weights(0, xq0, wq0, sc0, True)
+        hr0 = quantize(h0, E5M2)
+        xr0 = quantize(turn(packed_words(x0), False, True), E4M3)
+        dv0 = gradient(xr0, hr0, True)
+
+        x1, xq1 = heads_along_d(1)
+        for u, pair in enumerate((v_pair0, v_pair1)):
+            gather_pair(tails[1], u, pair, group(tail_list, 1))
+        wq1 = tails_along_d(1)
+        sc1 = scale_product(1)
+        h1 = weights(1, xq1, wq1, sc1, False)
+
+        wi0 = quantize(turn(gathered_words(tails[0]), False, False), E4M3)
+        hi0 = quantize(turn(packed_words(h0), True, False), E5M2)
+        du0 = gradient(wi0, hi0, False)
+
+        xr1 = quantize(turn(packed_words(x1), False, False), E4M3)
+        hr1 = quantize(h1, E5M2)
+        dv1 = gradient(xr1, hr1, True)
+        wi1 = quantize(turn(gathered_words(tails[1]), False, False), E4M3)
+        hi1 = quantize(turn(packed_words(h1), True, False), E5M2)
+        du1 = gradient(wi1, hi1, False)
+
+        sides = ((out_0, tail_list, (dv0, dv1)), (out_1, head_list, (du0, du1)))
+        windows = [[keep.tile([P, T], F32, name="window%d_%d" % (o, t)) for t in range(PACK)] for o in range(2)]
+        for o in range(2):
+            for t in range(PACK):
+                nc.vector.memset(windows[o][t][:], 0.0)
+        for b in range(B):
+            for o, (out, lst, grads) in enumerate(sides):
+                rows = out.rearrange("(p t) c -> p t c", t=PACK)
+                for t in range(PACK):
+                    nc.vector.tensor_copy(windows[o][t][:].indirect(group(lst, b)), grads[b][t][:])
+                    if b == B - 1:
+                        nc.sync.dma_start(rows[:, t, :], windows[o][t][:])

@@ -22,21 +22,33 @@ P = 128
 PACK = 4
 K = P * PACK
 LIST_COLS = K // 16
+BLOCK_BYTES = 4 * T
 
 
 def tile_attend_gmf_nce_vu_kernel(tc, uT, vT, y, us, ts, offs, uoffs, out_0, out_1):
     nc = tc.nc
     with ExitStack() as ctx:
         keep = ctx.enter_context(tc.tile_pool(name="keep", bufs=1))
-        big = ctx.enter_context(tc.tile_pool(name="big", bufs=7))
+        big = ctx.enter_context(tc.tile_pool(name="big", bufs=4))
+        shared = ctx.enter_context(tc.tile_pool(name="shared", bufs=1))
         pairs = ctx.enter_context(tc.tile_pool(name="pairs", bufs=3))
-        packed = ctx.enter_context(tc.tile_pool(name="packed", bufs=4))
-        turned = ctx.enter_context(tc.tile_pool(name="turned", bufs=2))
-        quant = ctx.enter_context(tc.tile_pool(name="quant", bufs=8))
-        staged = ctx.enter_context(tc.tile_pool(name="staged", bufs=8))
-        logit_ps = ctx.enter_context(tc.psum_pool(name="logit_ps", bufs=4))
-        turn_ps = ctx.enter_context(tc.psum_pool(name="turn_ps", bufs=2))
-        grad_ps = ctx.enter_context(tc.psum_pool(name="grad_ps", bufs=2))
+        psum = ctx.enter_context(tc.psum_pool(name="psum", bufs=1))
+
+        banks = [psum.tile([P, PACK, P], F32, name="bank%d" % j) for j in range(8)]
+        stages = [keep.tile([P, K], F32, name="staged%d" % j) for j in range(8)]
+        operands = [
+            (
+                keep.tile([P, K], U32, name="codes%d" % j, align_bytes=64),
+                keep.tile([P, K], U8, name="scales%d" % j, align_bytes=64),
+            )
+            for j in range(8)
+        ]
+
+        def take(ring):
+            first = ring[0]
+            ring.append(first)
+            ring.remove(first)
+            return first
 
         head_list = keep.tile([P, B * LIST_COLS], U16, name="head_list")
         tail_list = keep.tile([P, B * LIST_COLS], U16, name="tail_list")
@@ -44,9 +56,16 @@ def tile_attend_gmf_nce_vu_kernel(tc, uT, vT, y, us, ts, offs, uoffs, out_0, out
         ident = keep.tile([P, P], F32, name="ident")
         warm = keep.tile([P, 8], F32, name="warm")
         warm_out = keep.tile([P, 8], F32, name="warm_out")
+        gathered = [keep.tile([P, K * PACK], BF16, name="gathered%d" % j, align_bytes=64) for j in range(3)]
+        logits = keep.tile([P, PACK, R], F32, name="logits", align_bytes=64)
         make_identity(nc, ident[:])
-        nc.vector.memset(warm[:], 0.0)
+        nc.gpsimd.memset(warm[:], 0.0)
         nc.scalar.activation(warm_out[:], warm[:], SIGMOID)
+
+        def block(name, shape, place=None):
+            if place is None:
+                return big.tile(shape, F32, name=name, tag="block", align_bytes=64)
+            return shared.tile(shape, F32, name=name, align_bytes=64, offset=place * BLOCK_BYTES)
 
         def group(lst, b):
             return lst[:, b * LIST_COLS : (b + 1) * LIST_COLS]
@@ -54,8 +73,8 @@ def tile_attend_gmf_nce_vu_kernel(tc, uT, vT, y, us, ts, offs, uoffs, out_0, out
         def load_pair(table, u, cuts, name):
             rows = table.rearrange("(p u e) c -> p u e c", u=2, e=2)
             pair = pairs.tile([P, T, 2], BF16, name=name, tag="pair")
-            for c0, c1, on_vector in cuts:
-                raw = big.tile([P, 2, c1 - c0], F32, name="raw", tag="big")
+            for c0, c1, place, on_vector in cuts:
+                raw = block("raw", [P, 2, c1 - c0], place)
                 nc.sync.dma_start(raw[:], rows[:, u, :, c0:c1])
                 src = raw[:].rearrange("p e c -> p c e")
                 if on_vector:
@@ -64,20 +83,28 @@ def tile_attend_gmf_nce_vu_kernel(tc, uT, vT, y, us, ts, offs, uoffs, out_0, out
                     nc.scalar.activation(pair[:, c0:c1, :], src, COPY)
             return pair
 
-        def gather_pair(dst, u, pair, lst):
-            window = pair[:].rearrange("p c e -> p (c e)").bitcast(U32)
-            nc.vector.tensor_copy(dst[:, u, :].bitcast(U32), window.indirect(lst))
-
         def quantize(src, fmt):
-            codes = quant.tile([P, K], U32, name="codes", tag="codes", align_bytes=64)
-            scales = quant.tile([P, K], U8, name="scales", tag="scales", align_bytes=64)
-            nc.vector.quantize_mx(codes[:].bitcast(fmt), scales[:], src[:])
+            codes, scales = take(operands)
+            nc.vector.quantize_mx(codes[:].bitcast(fmt), scales[:], src)
             return codes, scales, fmt
 
-        def mx(dst, stationary, t, moving):
+        def gather(table_pairs, lst, dst):
+            for u, pair in enumerate(table_pairs):
+                window = pair[:].rearrange("p c e -> p (c e)").bitcast(U32)
+                nc.vector.tensor_copy(dst[:].bitcast(U32)[:, u * K : (u + 1) * K], window.indirect(lst))
+
+        def pack(dst, src):
+            nc.vector.tensor_copy(
+                dst[:].rearrange("p (s q u e) -> p q s u e", s=PACK, u=2, e=2),
+                src[:].rearrange("p (u q s e) -> p q s u e", u=2, s=PACK, e=2),
+            )
+            return quantize(dst[:], E4M3)
+
+        def product(stationary, t, moving):
             cols = slice(t * P, (t + 1) * P)
+            acc = take(banks)
             nc.tensor.matmul_mx(
-                dst,
+                acc[:].rearrange("p s q -> p (s q)"),
                 lhsT=stationary[0][:, cols].bitcast(stationary[2]),
                 lhsT_scale=stationary[1][:, cols],
                 rhs=moving[0][:].bitcast(moving[2]),
@@ -85,157 +112,168 @@ def tile_attend_gmf_nce_vu_kernel(tc, uT, vT, y, us, ts, offs, uoffs, out_0, out
                 start=True,
                 stop=True,
             )
+            return acc
 
-        def turn(words, natural, on_vector):
-            dst = turned.tile([P, K * PACK], BF16, name="turned", tag="turned", align_bytes=64)
+        def transposes(source):
+            bank = take(banks)
+            for s in range(PACK):
+                nc.tensor.transpose(bank[:, s, :], source(s), ident[:])
+            return bank
+
+        def turn(dst, tile, natural):
+            words = tile[:].bitcast(F32).rearrange("p (s q u) -> p u s q", s=PACK, u=2)
             for u in range(2):
-                bank = turn_ps.tile([P, PACK, P], F32, name="bank", tag="bank")
-                for s in range(PACK):
-                    nc.tensor.transpose(bank[:, s, :], words(u, s), ident[:])
+                bank = transposes(lambda s: words[:, u, s, :])
                 halves = bank[:].rearrange("q s p -> q (s p)").bitcast(BF16)
                 if natural:
                     src = halves.rearrange("q (s p e) -> q p e s", s=PACK, e=2)
-                    out = dst[:].rearrange("q (p u e s) -> q u p e s", u=2, e=2, s=PACK)[:, u]
+                    out = dst.rearrange("q (p u e s) -> q u p e s", u=2, e=2, s=PACK)[:, u]
                 else:
                     src = halves.rearrange("q (s p e) -> q e p s", s=PACK, e=2)
-                    out = dst[:].rearrange("q (u e p s) -> q u e p s", u=2, e=2, s=PACK)[:, u]
-                if on_vector:
-                    nc.vector.tensor_copy(out, src)
-                else:
-                    nc.scalar.copy(out, src)
+                    out = dst.rearrange("q (u e p s) -> q u e p s", u=2, e=2, s=PACK)[:, u]
+                nc.scalar.copy(out, src)
             return dst
 
-        def packed_words(tile):
-            words = tile[:].bitcast(F32).rearrange("p (s q u) -> p u s q", s=PACK, u=2)
-            return lambda u, s: words[:, u, s, :]
+        def halves_of(tile):
+            return tile[:].rearrange("p t i -> p (t i)").bitcast(BF16).rearrange("p (h x) -> p h x", h=2)
 
-        def gathered_words(tile):
-            words = tile[:].rearrange("p u x -> p (u x)").bitcast(F32).rearrange("p (u q s) -> p u s q", u=2, s=PACK)
-            return lambda u, s: words[:, u, s, :]
+        def in_list_order(dst):
+            return dst.rearrange("p (q s) -> p q s", s=PACK)
 
-        halves_cut = [(0, T // 2, False), (T // 2, T, False)]
-        last_cut = [(0, T // 2, False), (T // 2, 3 * T // 4, True), (3 * T // 4, T, True)]
+        def by_quad(bank):
+            return bank[:].rearrange("p s q -> p q s")
 
-        heads = [keep.tile([P, 2, 2 * K], BF16, name="heads%d" % b) for b in range(B)]
-        tails = [keep.tile([P, 2, 2 * K], BF16, name="tails%d" % b) for b in range(B)]
-
-        u_pair0 = load_pair(uT, 0, halves_cut, "u_pair0")
-        nc.sync.dma_start(head_list[:], uoffs)
-        nc.sync.dma_start(tail_list[:], offs)
-        nc.sync.dma_start(row_scale[:], us.rearrange("b (p t) o -> p b (t o)", t=PACK))
-        u_pair1 = load_pair(uT, 1, halves_cut, "u_pair1")
-        for u, pair in enumerate((u_pair0, u_pair1)):
-            for b in range(B):
-                gather_pair(heads[b], u, pair, group(head_list, b))
-        v_pair0 = load_pair(vT, 0, halves_cut, "v_pair0")
-        v_pair1 = load_pair(vT, 1, last_cut, "v_pair1")
-        tail_scale_all = big.tile([P, T], F32, name="tail_scale_all", tag="big")
-        nc.sync.dma_start(tail_scale_all[:], ts)
-        labels = []
-        for b in range(B):
-            lab = big.tile([P, PACK, N], F32, name="labels", tag="big")
-            nc.sync.dma_start(lab[:], y[b].rearrange("(p t) i -> p t i", t=PACK))
-            labels.append(lab)
-
-        def heads_along_d(b):
-            x = packed.tile([P, K * PACK], BF16, name="x", tag="packed", align_bytes=64)
-            nc.vector.tensor_copy(
-                x[:].rearrange("p (s q u e) -> p q s u e", s=PACK, u=2, e=2),
-                heads[b][:].rearrange("p u (q s e) -> p q s u e", s=PACK, e=2),
-            )
-            return x, quantize(x, E4M3)
-
-        def tails_along_d(b):
-            w = packed.tile([P, K * PACK], BF16, name="w", tag="packed", align_bytes=64)
-            nc.vector.tensor_copy(
-                w[:].rearrange("p (i u e) -> p i u e", u=2, e=2),
-                tails[b][:].rearrange("p u (i e) -> p i u e", e=2),
-            )
-            return quantize(w, E4M3)
-
-        def scale_product(b):
-            picked = keep.tile([P, N], F32, name="picked%d" % b)
-            nc.vector.tensor_copy(picked[:], tail_scale_all[:].indirect(group(tail_list, b)))
-            sc = big.tile([P, PACK, N], F32, name="sc", tag="big")
+        def scale_product(b, sc):
+            bank = transposes(lambda s: slot_scale[:, b, s : s + 1].to_broadcast([P, P]))
             for t in range(PACK):
-                nc.scalar.activation(sc[:, t, :], picked[:], COPY, scale=row_scale[:, b, t : t + 1])
-            return sc
+                nc.scalar.activation(in_list_order(sc[:, t, :]), by_quad(bank), COPY, scale=row_scale[:, b, t : t + 1])
 
-        def weights(b, xq, wq, sc, on_vector):
-            eng = nc.vector if on_vector else nc.gpsimd
-            z = big.tile([P, PACK, N], F32, name="z", tag="big")
+        def scaled_logits(b, xq, wq):
+            for s in range(PACK):
+                acc = product(wq, s, xq)
+                nc.scalar.activation(
+                    logits[:, s, :], acc[:].rearrange("q t p -> q (t p)"), COPY, scale=slot_scale[:, b, s : s + 1]
+                )
+
+        def probabilities(b, prob):
             for t in range(PACK):
-                acc = logit_ps.tile([P, N], F32, name="acc", tag="acc")
-                mx(acc[:], xq, t, wq)
-                if on_vector:
-                    nc.vector.tensor_tensor(z[:, t, :], acc[:], sc[:, t, :], MULT)
-                else:
-                    nc.scalar.copy(z[:, t, :], acc[:])
-                    nc.gpsimd.tensor_tensor(z[:, t, :], z[:, t, :], sc[:, t, :], MULT)
-                nc.scalar.activation(z[:, t, :], z[:, t, :], SIGMOID)
+                bank = transposes(lambda s: logits[:, s, t * P : (t + 1) * P])
+                nc.scalar.activation(
+                    in_list_order(prob[:, t, :]), by_quad(bank), SIGMOID, scale=row_scale[:, b, t : t + 1]
+                )
+
+        def new_weights(name):
+            h = keep.tile([P, K * PACK], BF16, name=name, align_bytes=64)
+            return h, h[:].rearrange("p (s q t) -> p q s t", s=PACK, t=PACK)
+
+        def by_slot(planes):
+            return planes.rearrange("p t (q s) -> p q s t", s=PACK)
+
+        def weights_on_vector(prob, labels, sc):
             for t in range(PACK):
-                eng.tensor_tensor(z[:, t, :], z[:, t, :], labels[b][:, t, :], SUBTRACT)
-            h = packed.tile([P, K * PACK], BF16, name="h", tag="packed", align_bytes=64)
-            eng.tensor_tensor(
-                h[:].rearrange("p (s q t) -> p q s t", s=PACK, t=PACK),
-                z[:].rearrange("p t (q s) -> p q s t", s=PACK),
-                sc[:].rearrange("p t (q s) -> p q s t", s=PACK),
-                MULT,
-            )
+                nc.vector.tensor_tensor(prob[:, t, :], prob[:, t, :], labels[:, t, :], SUBTRACT)
+            h, h_by_slot = new_weights("h0")
+            nc.vector.tensor_tensor(h_by_slot, by_slot(prob[:]), by_slot(sc[:]), MULT)
             return h
 
-        def gradient(stationary, moving, permuted):
-            tiles = []
-            for t in range(PACK):
-                acc = grad_ps.tile([P, K], F32, name="grad", tag="grad")
-                mx(acc[:], stationary, t, moving)
-                st = staged.tile([P, K], F32, name="staged", tag="staged")
-                if permuted:
-                    nc.scalar.copy(
-                        st[:].rearrange("p (q s) -> p q s", s=PACK), acc[:].rearrange("p (s q) -> p q s", s=PACK)
-                    )
-                else:
-                    nc.scalar.copy(st[:], acc[:])
-                tiles.append(st)
-            return tiles
+        def weights_on_gpsimd(prob, labels, sc):
+            planes = keep.tile([P, PACK, N], BF16, name="planes")
+            h, h_by_slot = new_weights("h1")
+            for c in range(2):
+                cols = slice(c * N // 2, (c + 1) * N // 2)
+                nc.gpsimd.tensor_tensor(prob[:, :, cols], prob[:, :, cols], labels[:, :, cols], SUBTRACT)
+                nc.gpsimd.tensor_tensor(planes[:, :, cols], prob[:, :, cols], sc[:, :, cols], MULT)
+                quads = slice(cols.start // PACK, cols.stop // PACK)
+                nc.scalar.copy(h_by_slot[:, quads], by_slot(planes[:])[:, quads])
+            return h
 
-        x0, xq0 = heads_along_d(0)
-        for u, pair in enumerate((v_pair0, v_pair1)):
-            gather_pair(tails[0], u, pair, group(tail_list, 0))
-        wq0 = tails_along_d(0)
-        sc0 = scale_product(0)
-        h0 = weights(0, xq0, wq0, sc0, True)
-        hr0 = quantize(h0, E5M2)
-        xr0 = quantize(turn(packed_words(x0), False, True), E4M3)
-        dv0 = gradient(xr0, hr0, True)
+        def gradient(o, b, t, stationary, moving, st=None):
+            acc = product(stationary, t, moving)
+            if st is None:
+                st = take(stages)[:]
+            if o == 0:
+                nc.scalar.copy(in_list_order(st), by_quad(acc))
+            else:
+                nc.scalar.copy(st, acc[:].rearrange("p s q -> p (s q)"))
+            out, lst = sides[o]
+            nc.vector.tensor_copy(windows[o][t][:].indirect(group(lst, b)), st)
+            if b == B - 1:
+                nc.sync.dma_start(out.rearrange("(p t) c -> p t c", t=PACK)[:, t, :], windows[o][t][:])
 
-        x1, xq1 = heads_along_d(1)
-        for u, pair in enumerate((v_pair0, v_pair1)):
-            gather_pair(tails[1], u, pair, group(tail_list, 1))
-        wq1 = tails_along_d(1)
-        sc1 = scale_product(1)
-        h1 = weights(1, xq1, wq1, sc1, False)
+        halves_cut = [(0, T // 2, None, False), (T // 2, T, None, False)]
+        last_cut = [(0, T // 2, 0, False), (T // 2, 3 * T // 4, None, True), (3 * T // 4, T, None, True)]
 
-        wi0 = quantize(turn(gathered_words(tails[0]), False, False), E4M3)
-        hi0 = quantize(turn(packed_words(h0), True, False), E5M2)
-        du0 = gradient(wi0, hi0, False)
-
-        xr1 = quantize(turn(packed_words(x1), False, False), E4M3)
-        hr1 = quantize(h1, E5M2)
-        dv1 = gradient(xr1, hr1, True)
-        wi1 = quantize(turn(gathered_words(tails[1]), False, False), E4M3)
-        hi1 = quantize(turn(packed_words(h1), True, False), E5M2)
-        du1 = gradient(wi1, hi1, False)
-
-        sides = ((out_0, tail_list, (dv0, dv1)), (out_1, head_list, (du0, du1)))
-        windows = [[keep.tile([P, T], F32, name="window%d_%d" % (o, t)) for t in range(PACK)] for o in range(2)]
-        for o in range(2):
-            for t in range(PACK):
-                nc.vector.memset(windows[o][t][:], 0.0)
+        tail_scale_row = block("tail_scale_row", [P, T], 1)
+        nc.vector.memset(tail_scale_row[:], 0.0)
+        u_pairs = [load_pair(uT, 0, halves_cut, "u_pair0")]
+        nc.sync.dma_start(tail_list[:], offs)
+        nc.sync.dma_start(head_list[:], uoffs)
+        nc.sync.dma_start(tail_scale_row[0:1, :], ts[0:1, :])
+        u_pairs.append(load_pair(uT, 1, [halves_cut[0], (T // 2, T, 3, False)], "u_pair1"))
+        v_pairs = [load_pair(vT, 0, halves_cut, "v_pair0"), load_pair(vT, 1, last_cut, "v_pair1")]
+        nc.sync.dma_start(row_scale[:], us.rearrange("b (p t) o -> p b (t o)", t=PACK))
+        labels = []
         for b in range(B):
-            for o, (out, lst, grads) in enumerate(sides):
-                rows = out.rearrange("(p t) c -> p t c", t=PACK)
-                for t in range(PACK):
-                    nc.vector.tensor_copy(windows[o][t][:].indirect(group(lst, b)), grads[b][t][:])
-                    if b == B - 1:
-                        nc.sync.dma_start(rows[:, t, :], windows[o][t][:])
+            labels.append(block("labels", [P, PACK, N]))
+            nc.sync.dma_start(labels[b][:], y[b].rearrange("(p t) i -> p t i", t=PACK))
+
+        picked = keep.tile([P, B * N], F32, name="picked")
+        nc.vector.tensor_copy(picked[:], tail_scale_row[:].indirect(tail_list[:]))
+        slot_scale = block("slot_scale", [P, B, PACK], 3)
+        picked_by_slot = picked[:].rearrange("p (b q s) -> p b s q", b=B, s=PACK)
+        for b in range(B):
+            bank = transposes(lambda s: picked_by_slot[:, b, s, :])
+            nc.vector.tensor_copy(slot_scale[:, b, :], bank[:, :, 0])
+
+        sides = ((out_0, tail_list), (out_1, head_list))
+        windows = [[keep.tile([P, T], F32, name="window%d_%d" % (o, t)) for t in range(PACK - o)] for o in range(2)]
+        for window in windows[0] + windows[1]:
+            nc.vector.memset(window[:], 0.0)
+
+        x0, w0, w1 = [keep.tile([P, K * PACK], BF16, name=name, align_bytes=64) for name in ("x0", "w0", "w1")]
+        gather(u_pairs, group(head_list, 0), gathered[0])
+        xq0 = pack(x0, gathered[0])
+        gather(v_pairs, group(tail_list, 0), gathered[2])
+        wq0 = pack(w0, gathered[2])
+        gather(u_pairs, group(head_list, 1), gathered[1])
+        prob1 = block("prob1", [P, PACK, N], 0)
+        x0_turned = turn(halves_of(prob1)[:, 0, :], x0, False)
+
+        prob0 = block("prob0", [P, PACK, N], 1)
+        sc0 = block("sc0", [P, PACK, N], 2)
+        scale_product(0, sc0)
+        scaled_logits(0, xq0, wq0)
+        probabilities(0, prob0)
+        h0 = weights_on_vector(prob0, labels[0], sc0)
+        hr0 = quantize(h0[:], E5M2)
+        xr0 = quantize(x0_turned, E4M3)
+        x1 = gathered[2]
+        xq1 = pack(x1, gathered[1])
+        gather(v_pairs, group(tail_list, 1), gathered[1])
+        wq1 = pack(w1, gathered[1])
+        xr1 = quantize(turn(halves_of(prob1)[:, 1, :], x1, False), E4M3)
+        wi0 = quantize(turn(halves_of(logits)[:, 0, :], w0, False), E4M3)
+        windows[1].append(block("window1_3", [P, T], 2))
+        nc.vector.memset(windows[1][3][:], 0.0)
+
+        gradient(0, 0, 0, xr0, hr0)
+        hi0 = quantize(turn(halves_of(prob1)[:, 0, :], h0, True), E5M2)
+        gradient(0, 0, 1, xr0, hr0)
+        scaled_logits(1, xq1, wq1)
+        gradient(0, 0, 2, xr0, hr0)
+        sc1 = block("sc1", [P, PACK, N], 1)
+        scale_product(1, sc1)
+        probabilities(1, prob1)
+        gradient(0, 0, 3, xr0, hr0)
+        h1 = weights_on_gpsimd(prob1, labels[1], sc1)
+        for t in range(PACK - 1):
+            gradient(1, 0, t, wi0, hi0)
+        hr1 = quantize(h1[:], E5M2)
+        gradient(1, 0, PACK - 1, wi0, hi0, sc1[:, 0, :])
+        gradient(0, 1, 0, xr1, hr1)
+        hi1 = quantize(turn(halves_of(labels[1])[:, 0, :], h1, True), E5M2)
+        wi1 = quantize(turn(halves_of(sc1)[:, 1, :], w1, False), E4M3)
+        for t in range(1, PACK):
+            gradient(0, 1, t, xr1, hr1)
+        for t in range(PACK):
+            gradient(1, 1, t, wi1, hi1)

@@ -54,13 +54,9 @@ def tile_attend_gmf_nce_vu_kernel(tc, uT, vT, y, us, ts, offs, uoffs, out_0, out
         tail_list = keep.tile([P, B * LIST_COLS], U16, name="tail_list")
         row_scale = keep.tile([P, B, PACK], F32, name="row_scale")
         ident = keep.tile([P, P], F32, name="ident")
-        warm = keep.tile([P, 8], F32, name="warm")
-        warm_out = keep.tile([P, 8], F32, name="warm_out")
         gathered = [keep.tile([P, K * PACK], BF16, name="gathered%d" % j, align_bytes=64) for j in range(3)]
         logits = keep.tile([P, PACK, R], F32, name="logits", align_bytes=64)
         make_identity(nc, ident[:])
-        nc.gpsimd.memset(warm[:], 0.0)
-        nc.scalar.activation(warm_out[:], warm[:], SIGMOID)
 
         def block(name, shape, place=None):
             if place is None:

@@ -14,262 +14,384 @@ U8 = mybir.dt.uint8
 E4M3 = mybir.dt.float8_e4m3fn_x4
 E5M2 = mybir.dt.float8_e5m2_x4
 MULT = mybir.AluOpType.mult
+ADD = mybir.AluOpType.add
 SUBTRACT = mybir.AluOpType.subtract
 COPY = mybir.ActivationFunctionType.Copy
 SIGMOID = mybir.ActivationFunctionType.Sigmoid
+TANH = mybir.ActivationFunctionType.Tanh
 
 P = 128
 PACK = 4
 K = P * PACK
+HALF = K // 2
+QUADS = HALF // PACK
 LIST_COLS = K // 16
-BLOCK_BYTES = 4 * T
+KIB = 1024
 
 
 def tile_attend_gmf_nce_vu_kernel(tc, uT, vT, y, us, ts, offs, uoffs, out_0, out_1):
     nc = tc.nc
     with ExitStack() as ctx:
         keep = ctx.enter_context(tc.tile_pool(name="keep", bufs=1))
-        big = ctx.enter_context(tc.tile_pool(name="big", bufs=4))
         shared = ctx.enter_context(tc.tile_pool(name="shared", bufs=1))
-        pairs = ctx.enter_context(tc.tile_pool(name="pairs", bufs=3))
         psum = ctx.enter_context(tc.psum_pool(name="psum", bufs=1))
 
         banks = [psum.tile([P, PACK, P], F32, name="bank%d" % j) for j in range(8)]
-        stages = [keep.tile([P, K], F32, name="staged%d" % j) for j in range(8)]
-        operands = [
-            (
-                keep.tile([P, K], U32, name="codes%d" % j, align_bytes=64),
-                keep.tile([P, K], U8, name="scales%d" % j, align_bytes=64),
-            )
-            for j in range(8)
-        ]
 
-        def take(ring):
-            first = ring[0]
-            ring.append(first)
-            ring.remove(first)
-            return first
+        def held(name, shape, dtype=F32):
+            return keep.tile(shape, dtype, name=name, align_bytes=64)
+
+        def placed(name, shape, kib, dtype=F32):
+            return shared.tile(shape, dtype, name=name, align_bytes=64, offset=int(kib * KIB))
+
+        def flat(bank):
+            return bank[:].rearrange("p s q -> p (s q)")
 
         head_list = keep.tile([P, B * LIST_COLS], U16, name="head_list")
         tail_list = keep.tile([P, B * LIST_COLS], U16, name="tail_list")
-        row_scale = keep.tile([P, B, PACK], F32, name="row_scale")
-        ident = keep.tile([P, P], F32, name="ident")
-        gathered = [keep.tile([P, K * PACK], BF16, name="gathered%d" % j, align_bytes=64) for j in range(3)]
-        logits = keep.tile([P, PACK, R], F32, name="logits", align_bytes=64)
+        row_scale = held("row_scale", [P, B, PACK])
+        half_scale = held("half_scale", [P, PACK])
+        slot_scale = [held("slot_scale%d" % b, [P, PACK]) for b in range(B)]
+        ident = held("ident", [P, P])
+        operands = [(held("codes%d" % j, [P, K], U32), held("scales%d" % j, [P, K], U8)) for j in range(6)]
+        xq, wq, xr0, hr0 = operands[0:2], operands[2:4], operands[4], operands[5]
         make_identity(nc, ident[:])
+        nc.gpsimd.memset(hr0[0][:, HALF:K], 0)
+        nc.gpsimd.memset(hr0[1][:, HALF:K], 0)
 
-        def block(name, shape, place=None):
-            if place is None:
-                return big.tile(shape, F32, name=name, tag="block", align_bytes=64)
-            return shared.tile(shape, F32, name=name, align_bytes=64, offset=place * BLOCK_BYTES)
+        def entries(lst, first, count):
+            return lst[:, first // 16 : (first + count) // 16]
 
-        def group(lst, b):
-            return lst[:, b * LIST_COLS : (b + 1) * LIST_COLS]
-
-        def load_pair(table, u, cuts, name):
+        def load_pair(table, u, name, kib, cuts):
             rows = table.rearrange("(p u e) c -> p u e c", u=2, e=2)
-            pair = pairs.tile([P, T, 2], BF16, name=name, tag="pair")
-            for c0, c1, place, on_vector in cuts:
-                raw = block("raw", [P, 2, c1 - c0], place)
+            pair = placed(name, [P, T, 2], kib, BF16)
+            late = []
+            for c0, c1, raw_kib, on_vector in cuts:
+                raw = placed("%s_raw%d" % (name, c0), [P, 2, c1 - c0], raw_kib)
                 nc.sync.dma_start(raw[:], rows[:, u, :, c0:c1])
                 src = raw[:].rearrange("p e c -> p c e")
                 if on_vector:
-                    nc.vector.tensor_copy(pair[:, c0:c1, :], src)
+                    late.append((pair[:, c0:c1, :], src))
                 else:
                     nc.scalar.activation(pair[:, c0:c1, :], src, COPY)
-            return pair
+            return pair, late
 
-        def quantize(src, fmt):
-            codes, scales = take(operands)
-            nc.vector.quantize_mx(codes[:].bitcast(fmt), scales[:], src)
-            return codes, scales, fmt
+        def gather(pair, lst, first, count, dst):
+            window = pair[:].rearrange("p c e -> p (c e)").bitcast(U32)
+            nc.vector.tensor_copy(dst, window.indirect(entries(lst, first, count)))
 
-        def gather(table_pairs, lst, dst):
-            for u, pair in enumerate(table_pairs):
-                window = pair[:].rearrange("p c e -> p (c e)").bitcast(U32)
-                nc.vector.tensor_copy(dst[:].bitcast(U32)[:, u * K : (u + 1) * K], window.indirect(lst))
-
-        def pack(dst, src):
+        def pack(dst, planes, q0, q1):
             nc.vector.tensor_copy(
-                dst[:].rearrange("p (s q u e) -> p q s u e", s=PACK, u=2, e=2),
-                src[:].rearrange("p (u q s e) -> p q s u e", u=2, s=PACK, e=2),
+                dst[:].rearrange("p (s q u e) -> p q s u e", s=PACK, u=2, e=2)[:, q0:q1],
+                planes.rearrange("p u (q s e) -> p q s u e", s=PACK, e=2)[:, q0:q1],
             )
-            return quantize(dst[:], E4M3)
 
-        def product(stationary, t, moving):
+        def quantize(operand, src, fmt):
+            nc.vector.quantize_mx(operand[0][:].bitcast(fmt), operand[1][:], src)
+
+        def quantize_half(operand, src, fmt, half):
+            for s in range(PACK):
+                cols = slice((half * PACK + s) * QUADS, (half * PACK + s + 1) * QUADS)
+                first = s * K + half * HALF
+                nc.vector.quantize_mx(operand[0][:, cols].bitcast(fmt), operand[1][:, cols], src[:, first : first + HALF])
+
+        def product(bank, stationary, t, moving, moving_fmt):
             cols = slice(t * P, (t + 1) * P)
-            acc = take(banks)
             nc.tensor.matmul_mx(
-                acc[:].rearrange("p s q -> p (s q)"),
-                lhsT=stationary[0][:, cols].bitcast(stationary[2]),
+                flat(bank),
+                lhsT=stationary[0][:, cols].bitcast(E4M3),
                 lhsT_scale=stationary[1][:, cols],
-                rhs=moving[0][:].bitcast(moving[2]),
+                rhs=moving[0][:].bitcast(moving_fmt),
                 rhs_scale=moving[1][:],
                 start=True,
                 stop=True,
             )
-            return acc
 
-        def transposes(source):
-            bank = take(banks)
+        def transposes(bank, source):
             for s in range(PACK):
                 nc.tensor.transpose(bank[:, s, :], source(s), ident[:])
-            return bank
 
-        def turn(dst, tile, natural):
+        def turn(dst, tile, natural, two_banks):
             words = tile[:].bitcast(F32).rearrange("p (s q u) -> p u s q", s=PACK, u=2)
-            for u in range(2):
-                bank = transposes(lambda s: words[:, u, s, :])
-                halves = bank[:].rearrange("q s p -> q (s p)").bitcast(BF16)
+            for u, bank in enumerate(two_banks):
+                transposes(bank, lambda s: words[:, u, s, :])
+                halves = flat(bank).bitcast(BF16)
                 if natural:
                     src = halves.rearrange("q (s p e) -> q p e s", s=PACK, e=2)
-                    out = dst.rearrange("q (p u e s) -> q u p e s", u=2, e=2, s=PACK)[:, u]
+                    out = dst[:].rearrange("q (p u e s) -> q u p e s", u=2, e=2, s=PACK)[:, u]
                 else:
                     src = halves.rearrange("q (s p e) -> q e p s", s=PACK, e=2)
-                    out = dst.rearrange("q (u e p s) -> q u e p s", u=2, e=2, s=PACK)[:, u]
+                    out = dst[:].rearrange("q (u e p s) -> q u e p s", u=2, e=2, s=PACK)[:, u]
                 nc.scalar.copy(out, src)
-            return dst
-
-        def halves_of(tile):
-            return tile[:].rearrange("p t i -> p (t i)").bitcast(BF16).rearrange("p (h x) -> p h x", h=2)
 
         def in_list_order(dst):
             return dst.rearrange("p (q s) -> p q s", s=PACK)
 
-        def by_quad(bank):
-            return bank[:].rearrange("p s q -> p q s")
+        def by_quad(dealt):
+            return dealt.rearrange("p (s q) -> p q s", s=PACK)
 
-        def scale_product(b, sc):
-            bank = transposes(lambda s: slot_scale[:, b, s : s + 1].to_broadcast([P, P]))
-            for t in range(PACK):
-                nc.scalar.activation(in_list_order(sc[:, t, :]), by_quad(bank), COPY, scale=row_scale[:, b, t : t + 1])
-
-        def scaled_logits(b, xq, wq):
-            for s in range(PACK):
-                acc = product(wq, s, xq)
-                nc.scalar.activation(
-                    logits[:, s, :], acc[:].rearrange("q t p -> q (t p)"), COPY, scale=slot_scale[:, b, s : s + 1]
-                )
-
-        def probabilities(b, prob):
-            for t in range(PACK):
-                bank = transposes(lambda s: logits[:, s, t * P : (t + 1) * P])
-                nc.scalar.activation(
-                    in_list_order(prob[:, t, :]), by_quad(bank), SIGMOID, scale=row_scale[:, b, t : t + 1]
-                )
-
-        def new_weights(name):
-            h = keep.tile([P, K * PACK], BF16, name=name, align_bytes=64)
-            return h, h[:].rearrange("p (s q t) -> p q s t", s=PACK, t=PACK)
+        def scaled_logits(bank, b, j):
+            product(bank, wq[b], j, xq[b], E4M3)
+            nc.scalar.activation(logits[b][:, j, :], flat(bank), COPY, scale=slot_scale[b][:, j : j + 1])
 
         def by_slot(planes):
             return planes.rearrange("p t (q s) -> p q s t", s=PACK)
 
-        def weights_on_vector(prob, labels, sc):
-            for t in range(PACK):
-                nc.vector.tensor_tensor(prob[:, t, :], prob[:, t, :], labels[:, t, :], SUBTRACT)
-            h, h_by_slot = new_weights("h0")
-            nc.vector.tensor_tensor(h_by_slot, by_slot(prob[:]), by_slot(sc[:]), MULT)
-            return h
+        def dealt_slots(h):
+            return h[:].rearrange("p (s q t) -> p q s t", s=PACK, t=PACK)
 
-        def weights_on_gpsimd(prob, labels, sc):
-            planes = keep.tile([P, PACK, N], BF16, name="planes")
-            h, h_by_slot = new_weights("h1")
-            for c in range(2):
-                cols = slice(c * N // 2, (c + 1) * N // 2)
-                nc.gpsimd.tensor_tensor(prob[:, :, cols], prob[:, :, cols], labels[:, :, cols], SUBTRACT)
-                nc.gpsimd.tensor_tensor(planes[:, :, cols], prob[:, :, cols], sc[:, :, cols], MULT)
-                quads = slice(cols.start // PACK, cols.stop // PACK)
-                nc.scalar.copy(h_by_slot[:, quads], by_slot(planes[:])[:, quads])
-            return h
-
-        def gradient(o, b, t, stationary, moving, st=None):
-            acc = product(stationary, t, moving)
-            if st is None:
-                st = take(stages)[:]
-            if o == 0:
-                nc.scalar.copy(in_list_order(st), by_quad(acc))
-            else:
-                nc.scalar.copy(st, acc[:].rearrange("p s q -> p (s q)"))
+        def scatter(o, t, first, count, staged, last):
             out, lst = sides[o]
-            nc.vector.tensor_copy(windows[o][t][:].indirect(group(lst, b)), st)
-            if b == B - 1:
+            nc.vector.tensor_copy(windows[o][t][:].indirect(entries(lst, first, count)), staged)
+            if last:
                 nc.sync.dma_start(out.rearrange("(p t) c -> p t c", t=PACK)[:, t, :], windows[o][t][:])
 
-        halves_cut = [(0, T // 2, None, False), (T // 2, T, None, False)]
-        last_cut = [(0, T // 2, 0, False), (T // 2, 3 * T // 4, None, True), (3 * T // 4, T, None, True)]
+        def tail_gradient(bank, t, xr, hr, cols, first, staged, last):
+            product(bank, xr, t, hr, E5M2)
+            nc.scalar.copy(in_list_order(staged[:]), by_quad(flat(bank)[:, cols]))
+            scatter(0, t, first, cols.stop - cols.start, staged[:], last)
 
-        tail_scale_row = block("tail_scale_row", [P, T], 1)
-        nc.vector.memset(tail_scale_row[:], 0.0)
-        u_pairs = [load_pair(uT, 0, halves_cut, "u_pair0")]
-        nc.sync.dma_start(tail_list[:], offs)
-        nc.sync.dma_start(head_list[:], uoffs)
-        nc.sync.dma_start(tail_scale_row[0:1, :], ts[0:1, :])
-        u_pairs.append(load_pair(uT, 1, [halves_cut[0], (T // 2, T, 3, False)], "u_pair1"))
-        v_pairs = [load_pair(vT, 0, halves_cut, "v_pair0"), load_pair(vT, 1, last_cut, "v_pair1")]
-        nc.sync.dma_start(row_scale[:], us.rearrange("b (p t) o -> p b (t o)", t=PACK))
-        labels = []
-        for b in range(B):
-            labels.append(block("labels", [P, PACK, N]))
-            nc.sync.dma_start(labels[b][:], y[b].rearrange("(p t) i -> p t i", t=PACK))
-
-        picked = keep.tile([P, B * N], F32, name="picked")
-        nc.vector.tensor_copy(picked[:], tail_scale_row[:].indirect(tail_list[:]))
-        slot_scale = block("slot_scale", [P, B, PACK], 3)
-        picked_by_slot = picked[:].rearrange("p (b q s) -> p b s q", b=B, s=PACK)
-        for b in range(B):
-            bank = transposes(lambda s: picked_by_slot[:, b, s, :])
-            nc.vector.tensor_copy(slot_scale[:, b, :], bank[:, :, 0])
+        def head_gradient(bank, t, wi, hi, first, staged, last):
+            product(bank, wi, t, hi, E5M2)
+            nc.scalar.copy(staged[:], flat(bank))
+            scatter(1, t, first, K, staged[:], last)
 
         sides = ((out_0, tail_list), (out_1, head_list))
-        windows = [[keep.tile([P, T], F32, name="window%d_%d" % (o, t)) for t in range(PACK - o)] for o in range(2)]
-        for window in windows[0] + windows[1]:
+        tail_scale_row = placed("tail_scale_row", [P, T], 98)
+        nc.sync.dma_start(tail_scale_row[P - 1 : P, :], ts[0:1, :])
+        nc.sync.dma_start(tail_list[:], offs)
+        nc.vector.memset(tail_scale_row[0 : P - 1, :], 0.0)
+        windows = [[held("window0_%d" % t, [P, T]) for t in range(PACK)], []]
+        nc.vector.memset(windows[0][0][:], 0.0)
+        picked = placed("picked", [P, B * N], 72)
+        dealt = placed("dealt", [P, N], 76)
+        nc.vector.tensor_copy(picked[:], tail_scale_row[:].indirect(tail_list[:]))
+        nc.vector.tensor_copy(
+            dealt[:].rearrange("p (h s q) -> p h s q", h=2, s=PACK),
+            picked[:, 0:N].rearrange("p (h q s) -> p h s q", h=2, s=PACK),
+        )
+        transposes(banks[0], lambda j: dealt[:, j * P : (j + 1) * P])
+        transposes(banks[1], lambda s: picked[:, N : 2 * N].rearrange("p (q s) -> p s q", s=PACK)[:, s, :])
+        for window in windows[0][1:]:
             nc.vector.memset(window[:], 0.0)
 
-        x0, w0, w1 = [keep.tile([P, K * PACK], BF16, name=name, align_bytes=64) for name in ("x0", "w0", "w1")]
-        gather(u_pairs, group(head_list, 0), gathered[0])
-        xq0 = pack(x0, gathered[0])
-        gather(v_pairs, group(tail_list, 0), gathered[2])
-        wq0 = pack(w0, gathered[2])
-        gather(u_pairs, group(head_list, 1), gathered[1])
-        prob1 = block("prob1", [P, PACK, N], 0)
-        x0_turned = turn(halves_of(prob1)[:, 0, :], x0, False)
+        u_pair0, unused = load_pair(uT, 0, "u_pair0", 40, [(0, T // 2, 0, False), (T // 2, T, 64, False)])
+        nc.sync.dma_start(head_list[:], uoffs)
+        nc.sync.dma_start(row_scale[:], us.rearrange("b (p t) o -> p b (t o)", t=PACK))
+        u_pair1, early_casts = load_pair(
+            uT, 1, "u_pair1", 48, [(0, 1024, 16, False), (1024, 1536, 24, False), (1536, T, 106, True)]
+        )
+        v_pair0, unused = load_pair(vT, 0, "v_pair0", 32, [(0, T // 2, 0, False), (T // 2, T, 8, False)])
+        v_pair1, late_casts = load_pair(
+            vT, 1, "v_pair1", 56, [(0, 1024, 16, False), (1024, 1408, 117, False), (1408, 1792, 24, True), (1792, T, 28, True)]
+        )
+        labels = []
+        for b in range(B):
+            labels.append(placed("labels%d" % b, [P, PACK, N], 8 * b))
+            nc.sync.dma_start(labels[b][:], y[b].rearrange("(p t) i -> p t i", t=PACK))
 
-        prob0 = block("prob0", [P, PACK, N], 1)
-        sc0 = block("sc0", [P, PACK, N], 2)
-        scale_product(0, sc0)
-        scaled_logits(0, xq0, wq0)
-        probabilities(0, prob0)
-        h0 = weights_on_vector(prob0, labels[0], sc0)
-        hr0 = quantize(h0[:], E5M2)
-        xr0 = quantize(x0_turned, E4M3)
-        x1 = gathered[2]
-        xq1 = pack(x1, gathered[1])
-        gather(v_pairs, group(tail_list, 1), gathered[1])
-        wq1 = pack(w1, gathered[1])
-        xr1 = quantize(turn(halves_of(prob1)[:, 1, :], x1, False), E4M3)
-        wi0 = quantize(turn(halves_of(logits)[:, 0, :], w0, False), E4M3)
-        windows[1].append(block("window1_3", [P, T], 2))
-        nc.vector.memset(windows[1][3][:], 0.0)
+        heads = placed("heads", [P, 2 * B * K], 80, U32)
+        tails = placed("tails", [P, 3 * K], 88, U32)
+        head_planes = heads[:].bitcast(BF16).rearrange("p (u b x) -> p b u x", u=2, b=B)
+        tail_planes = tails[:].bitcast(BF16).rearrange("p (u x) -> p u x", u=3)
+        gather(u_pair0, head_list, 0, B * K, heads[:, 0 : B * K])
+        for dst, src in early_casts:
+            nc.vector.tensor_copy(dst, src)
+        for t, kib in enumerate((64, 106)):
+            windows[1].append(placed("window1_%d" % t, [P, T], kib))
+            nc.gpsimd.memset(windows[1][t][:], 0.0)
+        gather(u_pair1, head_list, 0, B * K, heads[:, B * K : 2 * B * K])
+        for b in range(B):
+            nc.vector.tensor_copy(slot_scale[b][:], banks[b][:, :, P - 1])
+        nc.vector.tensor_scalar(half_scale[:], row_scale[:, 0, :], 0.5, None, MULT)
+        x = [held("x%d" % b, [P, K * PACK], BF16) for b in range(B)]
+        w = [held("w0", [P, K * PACK], BF16)]
+        for b in range(B):
+            pack(x[b], head_planes[:, b], 0, P)
+        for b in range(B):
+            quantize(xq[b], x[b][:], E4M3)
+        gather(v_pair0, tail_list, 0, B * K, tails[:, 0 : B * K])
 
-        gradient(0, 0, 0, xr0, hr0)
-        hi0 = quantize(turn(halves_of(prob1)[:, 0, :], h0, True), E5M2)
-        gradient(0, 0, 1, xr0, hr0)
-        scaled_logits(1, xq1, wq1)
-        gradient(0, 0, 2, xr0, hr0)
-        sc1 = block("sc1", [P, PACK, N], 1)
-        scale_product(1, sc1)
-        probabilities(1, prob1)
-        gradient(0, 0, 3, xr0, hr0)
-        h1 = weights_on_gpsimd(prob1, labels[1], sc1)
-        for t in range(PACK - 1):
-            gradient(1, 0, t, wi0, hi0)
-        hr1 = quantize(h1[:], E5M2)
-        gradient(1, 0, PACK - 1, wi0, hi0, sc1[:, 0, :])
-        gradient(0, 1, 0, xr1, hr1)
-        hi1 = quantize(turn(halves_of(labels[1])[:, 0, :], h1, True), E5M2)
-        wi1 = quantize(turn(halves_of(sc1)[:, 1, :], w1, False), E4M3)
-        for t in range(1, PACK):
-            gradient(0, 1, t, xr1, hr1)
+        x0_turned = placed("x0_turned", [P, K * PACK], 114, BF16)
+        turn(x0_turned, x[0], False, banks[3:5])
+        sc_a = placed("sc_a", [P, PACK, HALF], 119)
+        for j in range(2):
+            nc.tensor.transpose(banks[2][:, j, :], slot_scale[0][:, j : j + 1].to_broadcast([P, P]), ident[:])
         for t in range(PACK):
-            gradient(1, 1, t, wi1, hi1)
+            nc.scalar.activation(sc_a[:, t, :], flat(banks[2])[:, 0:HALF], COPY, scale=half_scale[:, t : t + 1])
+
+        for dst, src in late_casts:
+            nc.vector.tensor_copy(dst, src)
+        for half in range(2):
+            gather(v_pair1, tail_list, half * HALF, HALF, tails[:, 2 * K + half * HALF : 2 * K + (half + 1) * HALF])
+        for half in range(2):
+            pack(w[0], tail_planes[:, 0:3:2], half * QUADS, (half + 1) * QUADS)
+        for half in range(2):
+            quantize_half(wq[0], w[0], E4M3, half)
+
+        logits = [placed("logits%d" % b, [P, PACK, R], 48) for b in range(B)]
+        prob0 = placed("prob0", [P, PACK, N], 16)
+        for c in range(2):
+            rows = slice(c * HALF, (c + 1) * HALF)
+            for j in range(2):
+                nc.tensor.matmul_mx(
+                    flat(banks[c])[:, j * HALF : (j + 1) * HALF],
+                    lhsT=wq[0][0][:, j * P : (j + 1) * P].bitcast(E4M3),
+                    lhsT_scale=wq[0][1][:, j * P : (j + 1) * P],
+                    rhs=xq[0][0][:, rows].bitcast(E4M3),
+                    rhs_scale=xq[0][1][:, rows],
+                    start=True,
+                    stop=True,
+                )
+            for j in range(2):
+                nc.scalar.activation(
+                    logits[0][:, j, rows],
+                    flat(banks[c])[:, j * HALF : (j + 1) * HALF],
+                    COPY,
+                    scale=slot_scale[0][:, j : j + 1],
+                )
+        for t in range(PACK):
+            bank = banks[4 + t]
+            for j in range(2):
+                nc.tensor.transpose(bank[:, j, :], logits[0][:, j, t * P : (t + 1) * P], ident[:])
+            nc.scalar.activation(
+                in_list_order(prob0[:, t, 0:HALF]), by_quad(flat(bank)[:, 0:HALF]), TANH, scale=half_scale[:, t : t + 1]
+            )
+        for j in range(2, 4):
+            scaled_logits(banks[j], 0, j)
+
+        diff_a = placed("diff_a", [P, PACK, HALF], 94)
+        h0 = placed("h0", [P, K * PACK], 72, BF16)
+        for t in range(PACK):
+            nc.vector.scalar_tensor_tensor(
+                by_quad(diff_a[:, t, :]),
+                in_list_order(labels[0][:, t, 0:HALF]),
+                -2.0,
+                in_list_order(prob0[:, t, 0:HALF]),
+                MULT,
+                ADD,
+            )
+        nc.vector.scalar_tensor_tensor(
+            h0[:].rearrange("p (s q t) -> p s q t", s=PACK, t=PACK)[:, :, 0:QUADS, :],
+            diff_a[:].rearrange("p t (s q) -> p s q t", s=PACK),
+            1.0,
+            sc_a[:].rearrange("p t (s q) -> p s q t", s=PACK),
+            ADD,
+            MULT,
+        )
+        quantize_half(hr0, h0, E5M2, 0)
+
+        gather(v_pair1, tail_list, K, K, tails[:, 2 * K : 3 * K])
+        quantize(xr0, x0_turned[:], E4M3)
+        w.append(placed("w1", [P, K * PACK], 94, BF16))
+        pack(w[1], tail_planes[:, 1:3], 0, P)
+        quantize(wq[1], w[1][:], E4M3)
+
+        half_stages = [held("half_stage%d" % j, [P, HALF]) for j in range(8)]
+        for t in range(2):
+            tail_gradient(banks[4 + t], t, xr0, hr0, slice(0, HALF), 0, half_stages[t], False)
+
+        diff_b = placed("diff_b", [P, PACK, HALF], 88)
+        for t in range(PACK):
+            bank = banks[t // 2]
+            if t % 2 == 0:
+                for tt in range(2):
+                    for j in range(2):
+                        cols = slice((t + tt) * P, (t + tt + 1) * P)
+                        nc.tensor.transpose(bank[:, 2 * tt + j, :], logits[0][:, 2 + j, cols], ident[:])
+            nc.scalar.activation(
+                in_list_order(prob0[:, t, HALF:K]),
+                by_quad(flat(bank)[:, (t % 2) * HALF : (t % 2 + 1) * HALF]),
+                SIGMOID,
+                scale=row_scale[:, 0, t : t + 1],
+            )
+            nc.gpsimd.tensor_tensor(diff_b[:, t, :], prob0[:, t, HALF:K], labels[0][:, t, HALF:K], SUBTRACT)
+        sc_b = placed("sc_b", [P, PACK, HALF], 102)
+        for j in range(2):
+            nc.tensor.transpose(banks[4][:, j, :], slot_scale[0][:, 2 + j : 3 + j].to_broadcast([P, P]), ident[:])
+        for t in range(PACK):
+            nc.scalar.activation(
+                in_list_order(sc_b[:, t, :]), by_quad(flat(banks[4])[:, 0:HALF]), COPY, scale=row_scale[:, 0, t : t + 1]
+            )
+        for t in range(2, PACK):
+            tail_gradient(banks[4 + t], t, xr0, hr0, slice(0, HALF), 0, half_stages[t], False)
+        for c in range(2):
+            planes = placed("planes_b%d" % c, [P, PACK, P], 98 + c, BF16)
+            cols = slice(c * P, (c + 1) * P)
+            nc.gpsimd.tensor_tensor(planes[:], diff_b[:, :, cols], sc_b[:, :, cols], MULT)
+            quads = slice(QUADS + c * QUADS // 2, QUADS + (c + 1) * QUADS // 2)
+            nc.scalar.copy(dealt_slots(h0)[:, quads], by_slot(planes[:]))
+        quantize_half(hr0, h0, E5M2, 1)
+
+        w0_turned = placed("w0_turned", [P, K * PACK], 30, BF16)
+        turn(w0_turned, w[0], False, (banks[5], banks[4]))
+        wi0 = (placed("wi0_codes", [P, K], 99.5, U32), placed("wi0_scales", [P, K], 101.5, U8))
+        quantize(wi0, w0_turned[:], E4M3)
+        for t in range(2, PACK):
+            windows[1].append(placed("window1_%d" % t, [P, T], 8 + 8 * t))
+            nc.gpsimd.memset(windows[1][t][:], 0.0)
+
+        for t, bank in enumerate((2, 3, 1)):
+            tail_gradient(banks[bank], t, xr0, hr0, slice(HALF, K), HALF, half_stages[4 + t], False)
+        product(banks[0], xr0, PACK - 1, hr0, E5M2)
+        h0_turned = placed("h0_turned", [P, K * PACK], 0, BF16)
+        turn(h0_turned, h0, True, banks[2:4])
+        hi0 = wq[0]
+        quantize(hi0, h0_turned[:], E5M2)
+        late_stage = placed("late_stage_b", [P, HALF], 72)
+        nc.scalar.copy(in_list_order(late_stage[:]), by_quad(flat(banks[0])[:, HALF:K]))
+        scatter(0, PACK - 1, HALF, HALF, late_stage[:], False)
+
+        for s, bank in enumerate((6, 7, 4, 5)):
+            scaled_logits(banks[bank], 1, s)
+        prob1 = placed("prob1", [P, PACK, N], 16)
+        diff1 = placed("diff1", [P, PACK, N], 0)
+        stages = [held("stage%d" % j, [P, K]) for j in range(11)]
+        head_gradient(banks[1], 0, wi0, hi0, 0, stages[0], False)
+        for t, bank in enumerate((6, 7, 4, 5)):
+            transposes(banks[bank], lambda s: logits[1][:, s, t * P : (t + 1) * P])
+            nc.scalar.activation(
+                in_list_order(prob1[:, t, :]), by_quad(flat(banks[bank])), SIGMOID, scale=row_scale[:, 1, t : t + 1]
+            )
+            nc.gpsimd.tensor_tensor(diff1[:, t, :], prob1[:, t, :], labels[1][:, t, :], SUBTRACT)
+        head_gradient(banks[2], 1, wi0, hi0, 0, stages[1], False)
+
+        sc1 = placed("sc1", [P, PACK, N], 56)
+        transposes(banks[6], lambda s: slot_scale[1][:, s : s + 1].to_broadcast([P, P]))
+        for t in range(PACK):
+            nc.scalar.activation(
+                in_list_order(sc1[:, t, :]), by_quad(flat(banks[6])), COPY, scale=row_scale[:, 1, t : t + 1]
+            )
+        head_gradient(banks[3], 2, wi0, hi0, 0, stages[2], False)
+        product(banks[0], wi0, PACK - 1, hi0, E5M2)
+        nc.scalar.copy(half_stages[7][:], flat(banks[0])[:, 0:HALF])
+        scatter(1, PACK - 1, 0, HALF, half_stages[7][:], False)
+
+        h1 = placed("h1", [P, K * PACK], 119, BF16)
+        for c in range(2):
+            planes = placed("planes1_%d" % c, [P, PACK, HALF], 98 + 2 * c, BF16)
+            cols = slice(c * HALF, (c + 1) * HALF)
+            nc.gpsimd.tensor_tensor(planes[:], diff1[:, :, cols], sc1[:, :, cols], MULT)
+            nc.scalar.copy(dealt_slots(h1)[:, c * QUADS : (c + 1) * QUADS], by_slot(planes[:]))
+        x1_turned = placed("x1_turned", [P, K * PACK], 114, BF16)
+        turn(x1_turned, x[1], False, (banks[7], banks[4]))
+        w1_turned = placed("w1_turned", [P, K * PACK], 88, BF16)
+        turn(w1_turned, w[1], False, (banks[5], banks[1]))
+        xr1 = (placed("xr1_codes", [P, K], 0, U32), placed("xr1_scales", [P, K], 2, U8))
+        wi1 = (placed("wi1_codes", [P, K], 101, U32), placed("wi1_scales", [P, K], 103, U8))
+        hr1, hi1 = xq[1], wq[1]
+        quantize(xr1, x1_turned[:], E4M3)
+        quantize(hr1, h1[:], E5M2)
+        quantize(wi1, w1_turned[:], E4M3)
+        late_stage = placed("late_stage_h", [P, HALF], 100)
+        nc.scalar.copy(late_stage[:], flat(banks[0])[:, HALF:K])
+        scatter(1, PACK - 1, HALF, HALF, late_stage[:], False)
+
+        for t, bank in enumerate((2, 3, 6, 7)):
+            tail_gradient(banks[bank], t, xr1, hr1, slice(0, K), K, stages[3 + t], True)
+            if t == 1:
+                h1_turned = placed("h1_turned", [P, K * PACK], 80, BF16)
+                turn(h1_turned, h1, True, banks[4:6])
+                quantize(hi1, h1_turned[:], E5M2)
+        for t, bank in enumerate((1, 0, 2, 3)):
+            head_gradient(banks[bank], t, wi1, hi1, K, stages[7 + t], True)

@@ -56,8 +56,6 @@ def tile_attend_gmf_nce_vu_kernel(tc, uT, vT, y, us, ts, offs, uoffs, out_0, out
         operands = [(held("codes%d" % j, [P, K], U32), held("scales%d" % j, [P, K], U8)) for j in range(6)]
         xq, wq, xr0, hr0 = operands[0:2], operands[2:4], operands[4], operands[5]
         make_identity(nc, ident[:])
-        nc.gpsimd.memset(hr0[0][:, HALF:K], 0)
-        nc.gpsimd.memset(hr0[1][:, HALF:K], 0)
 
         def entries(lst, first, count):
             return lst[:, first // 16 : (first + count) // 16]
@@ -174,6 +172,8 @@ def tile_attend_gmf_nce_vu_kernel(tc, uT, vT, y, us, ts, offs, uoffs, out_0, out
         transposes(banks[1], lambda s: picked[:, N : 2 * N].rearrange("p (q s) -> p s q", s=PACK)[:, s, :])
         for window in windows[0][1:]:
             nc.vector.memset(window[:], 0.0)
+        nc.vector.memset(hr0[0][:, HALF:K], 0)
+        nc.vector.memset(hr0[1][:, HALF:K], 0)
 
         u_pair0, unused = load_pair(uT, 0, "u_pair0", 40, [(0, T // 2, 0, False), (T // 2, T, 64, False)])
         nc.sync.dma_start(head_list[:], uoffs)
@@ -283,6 +283,8 @@ def tile_attend_gmf_nce_vu_kernel(tc, uT, vT, y, us, ts, offs, uoffs, out_0, out
 
         gather(v_pair1, tail_list, K, K, tails[:, 2 * K : 3 * K])
         quantize(xr0, x0_turned[:], E4M3)
+        windows[1].append(placed("window1_2", [P, T], 56))
+        nc.vector.memset(windows[1][2][:], 0.0)
         w.append(placed("w1", [P, K * PACK], 94, BF16))
         pack(w[1], tail_planes[:, 1:3], 0, P)
         quantize(wq[1], w[1][:], E4M3)
@@ -327,9 +329,14 @@ def tile_attend_gmf_nce_vu_kernel(tc, uT, vT, y, us, ts, offs, uoffs, out_0, out
         turn(w0_turned, w[0], False, (banks[5], banks[4]))
         wi0 = (placed("wi0_codes", [P, K], 99.5, U32), placed("wi0_scales", [P, K], 101.5, U8))
         quantize(wi0, w0_turned[:], E4M3)
-        for t in range(2, PACK):
-            windows[1].append(placed("window1_%d" % t, [P, T], 8 + 8 * t))
-            nc.gpsimd.memset(windows[1][t][:], 0.0)
+        windows[1].append(placed("window1_3", [P, T], 24))
+        nc.gpsimd.memset(windows[1][3][:], 0.0)
+        slot_row = held("slot_row", [P, N])
+        transposes(banks[7], lambda s: slot_scale[1][:, s : s + 1].to_broadcast([P, P]))
+        nc.scalar.copy(in_list_order(slot_row[:]), by_quad(flat(banks[7])))
+        sc1 = placed("sc1", [P, PACK, N], 32)
+        for t in range(PACK):
+            nc.gpsimd.tensor_scalar(sc1[:, t, :], slot_row[:], row_scale[:, 1, t : t + 1], 0.0, MULT, ADD)
 
         for t, bank in enumerate((2, 3, 1)):
             tail_gradient(banks[bank], t, xr0, hr0, slice(HALF, K), HALF, half_stages[4 + t], False)
@@ -347,51 +354,53 @@ def tile_attend_gmf_nce_vu_kernel(tc, uT, vT, y, us, ts, offs, uoffs, out_0, out
         prob1 = placed("prob1", [P, PACK, N], 16)
         diff1 = placed("diff1", [P, PACK, N], 0)
         stages = [held("stage%d" % j, [P, K]) for j in range(11)]
-        head_gradient(banks[1], 0, wi0, hi0, 0, stages[0], False)
         for t, bank in enumerate((6, 7, 4, 5)):
             transposes(banks[bank], lambda s: logits[1][:, s, t * P : (t + 1) * P])
             nc.scalar.activation(
                 in_list_order(prob1[:, t, :]), by_quad(flat(banks[bank])), SIGMOID, scale=row_scale[:, 1, t : t + 1]
             )
             nc.gpsimd.tensor_tensor(diff1[:, t, :], prob1[:, t, :], labels[1][:, t, :], SUBTRACT)
+            if t == 1:
+                head_gradient(banks[1], 0, wi0, hi0, 0, stages[0], False)
         head_gradient(banks[2], 1, wi0, hi0, 0, stages[1], False)
 
-        sc1 = placed("sc1", [P, PACK, N], 56)
-        transposes(banks[6], lambda s: slot_scale[1][:, s : s + 1].to_broadcast([P, P]))
-        for t in range(PACK):
-            nc.scalar.activation(
-                in_list_order(sc1[:, t, :]), by_quad(flat(banks[6])), COPY, scale=row_scale[:, 1, t : t + 1]
-            )
         head_gradient(banks[3], 2, wi0, hi0, 0, stages[2], False)
         product(banks[0], wi0, PACK - 1, hi0, E5M2)
         nc.scalar.copy(half_stages[7][:], flat(banks[0])[:, 0:HALF])
         scatter(1, PACK - 1, 0, HALF, half_stages[7][:], False)
 
-        h1 = placed("h1", [P, K * PACK], 119, BF16)
-        for c in range(2):
-            planes = placed("planes1_%d" % c, [P, PACK, HALF], 98 + 2 * c, BF16)
-            cols = slice(c * HALF, (c + 1) * HALF)
-            nc.gpsimd.tensor_tensor(planes[:], diff1[:, :, cols], sc1[:, :, cols], MULT)
-            nc.scalar.copy(dealt_slots(h1)[:, c * QUADS : (c + 1) * QUADS], by_slot(planes[:]))
         x1_turned = placed("x1_turned", [P, K * PACK], 114, BF16)
         turn(x1_turned, x[1], False, (banks[7], banks[4]))
         w1_turned = placed("w1_turned", [P, K * PACK], 88, BF16)
         turn(w1_turned, w[1], False, (banks[5], banks[1]))
+        h1 = placed("h1", [P, K * PACK], 119, BF16)
+        planes = placed("planes1", [P, PACK, N], 102, BF16)
+        for c in range(PACK):
+            cols = slice(c * P, (c + 1) * P)
+            nc.gpsimd.tensor_tensor(planes[:, :, cols], diff1[:, :, cols], sc1[:, :, cols], MULT)
+            quads = slice(c * P // PACK, (c + 1) * P // PACK)
+            nc.scalar.copy(dealt_slots(h1)[:, quads], by_slot(planes[:])[:, quads])
         xr1 = (placed("xr1_codes", [P, K], 0, U32), placed("xr1_scales", [P, K], 2, U8))
-        wi1 = (placed("wi1_codes", [P, K], 101, U32), placed("wi1_scales", [P, K], 103, U8))
+        wi1 = (placed("wi1_codes", [P, K], 4, U32), placed("wi1_scales", [P, K], 6, U8))
         hr1, hi1 = xq[1], wq[1]
         quantize(xr1, x1_turned[:], E4M3)
-        quantize(hr1, h1[:], E5M2)
         quantize(wi1, w1_turned[:], E4M3)
-        late_stage = placed("late_stage_h", [P, HALF], 100)
+        quantize(hr1, h1[:], E5M2)
+        late_stage = placed("late_stage_h", [P, HALF], 32)
         nc.scalar.copy(late_stage[:], flat(banks[0])[:, HALF:K])
         scatter(1, PACK - 1, HALF, HALF, late_stage[:], False)
 
         for t, bank in enumerate((2, 3, 6, 7)):
             tail_gradient(banks[bank], t, xr1, hr1, slice(0, K), K, stages[3 + t], True)
             if t == 1:
-                h1_turned = placed("h1_turned", [P, K * PACK], 80, BF16)
-                turn(h1_turned, h1, True, banks[4:6])
-                quantize(hi1, h1_turned[:], E5M2)
+                h1_turned = placed("h1_turned", [P, 2 * K], 80)
+                words = planes[:].rearrange("p t i -> p (t i)").bitcast(F32).rearrange("p (t q u) -> p t u q", t=PACK, u=2)
+                for j in range(2):
+                    transposes(banks[4 + j], lambda a: words[:, 2 * j + a // 2, a % 2, :])
+                    nc.scalar.copy(
+                        h1_turned[:].rearrange("q (p j a) -> q j p a", j=2, a=PACK)[:, j],
+                        banks[4 + j][:].rearrange("q a p -> q p a"),
+                    )
+                quantize(hi1, h1_turned[:].bitcast(BF16), E5M2)
         for t, bank in enumerate((1, 0, 2, 3)):
             head_gradient(banks[bank], t, wi1, hi1, K, stages[7 + t], True)

@@ -109,17 +109,13 @@ def tile_attend_gmf_nce_vu_kernel(tc, uT, vT, y, us, ts, offs, uoffs, out_0, out
             for s in range(PACK):
                 nc.tensor.transpose(bank[:, s, :], source(s), ident[:])
 
-        def turn(dst, tile, natural, two_banks):
+        def turn(dst, tile, two_banks):
             words = tile[:].bitcast(F32).rearrange("p (s q u) -> p u s q", s=PACK, u=2)
             for u, bank in enumerate(two_banks):
                 transposes(bank, lambda s: words[:, u, s, :])
                 halves = flat(bank).bitcast(BF16)
-                if natural:
-                    src = halves.rearrange("q (s p e) -> q p e s", s=PACK, e=2)
-                    out = dst[:].rearrange("q (p u e s) -> q u p e s", u=2, e=2, s=PACK)[:, u]
-                else:
-                    src = halves.rearrange("q (s p e) -> q e p s", s=PACK, e=2)
-                    out = dst[:].rearrange("q (u e p s) -> q u e p s", u=2, e=2, s=PACK)[:, u]
+                src = halves.rearrange("q (s p e) -> q e p s", s=PACK, e=2)
+                out = dst[:].rearrange("q (u e p s) -> q u e p s", u=2, e=2, s=PACK)[:, u]
                 nc.scalar.copy(out, src)
 
         def in_list_order(dst):
@@ -132,11 +128,23 @@ def tile_attend_gmf_nce_vu_kernel(tc, uT, vT, y, us, ts, offs, uoffs, out_0, out
             product(bank, wq[b], j, xq[b], E4M3)
             nc.scalar.activation(logits[b][:, j, :], flat(bank), COPY, scale=slot_scale[b][:, j : j + 1])
 
-        def by_slot(planes):
-            return planes.rearrange("p t (q s) -> p q s t", s=PACK)
+        def interleaving(h, planes, cols):
+            quads = slice(cols.start // PACK, cols.stop // PACK)
+            return (
+                h.rearrange("p (q s t) -> p q t s", s=PACK, t=PACK),
+                planes[:].rearrange("p t (q s) -> p q t s", s=PACK)[:, quads],
+            )
 
-        def dealt_slots(h):
-            return h[:].rearrange("p (s q t) -> p q s t", s=PACK, t=PACK)
+        def quantize_slots(operand, h, cols):
+            nc.vector.quantize_mx(operand[0][:, cols].bitcast(E5M2), operand[1][:, cols], h)
+
+        def turn_planes(dst, planes, two_banks):
+            words = planes[:].rearrange("p t i -> p (t i)").bitcast(F32).rearrange("p (t q u) -> p t u q", t=PACK, u=2)
+            for j, bank in enumerate(two_banks):
+                transposes(bank, lambda a: words[:, 2 * j + a // 2, a % 2, :])
+                nc.scalar.copy(
+                    dst[:].rearrange("q (p j a) -> q j p a", j=2, a=PACK)[:, j], bank[:].rearrange("q a p -> q p a")
+                )
 
         def scatter(o, t, first, count, staged, last):
             out, lst = sides[o]
@@ -146,7 +154,7 @@ def tile_attend_gmf_nce_vu_kernel(tc, uT, vT, y, us, ts, offs, uoffs, out_0, out
 
         def tail_gradient(bank, t, xr, hr, cols, first, staged, last):
             product(bank, xr, t, hr, E5M2)
-            nc.scalar.copy(in_list_order(staged[:]), by_quad(flat(bank)[:, cols]))
+            nc.scalar.copy(staged[:], flat(bank)[:, cols])
             scatter(0, t, first, cols.stop - cols.start, staged[:], last)
 
         def head_gradient(bank, t, wi, hi, first, staged, last):
@@ -177,23 +185,23 @@ def tile_attend_gmf_nce_vu_kernel(tc, uT, vT, y, us, ts, offs, uoffs, out_0, out
 
         u_pair0, unused = load_pair(uT, 0, "u_pair0", 40, [(0, T // 2, 0, False), (T // 2, T, 64, False)])
         nc.sync.dma_start(head_list[:], uoffs)
-        nc.sync.dma_start(row_scale[:], us.rearrange("b (p t) o -> p b (t o)", t=PACK))
         u_pair1, early_casts = load_pair(
-            uT, 1, "u_pair1", 48, [(0, 1024, 16, False), (1024, 1536, 24, False), (1536, T, 106, True)]
+            uT, 1, "u_pair1", 48, [(0, 1024, 8, False), (1024, 1536, 24, False), (1536, T, 106, True)]
         )
-        v_pair0, unused = load_pair(vT, 0, "v_pair0", 32, [(0, T // 2, 0, False), (T // 2, T, 8, False)])
+        v_pair0, unused = load_pair(vT, 0, "v_pair0", 32, [(0, T // 2, 16, False), (T // 2, T, 123, False)])
         v_pair1, late_casts = load_pair(
-            vT, 1, "v_pair1", 56, [(0, 1024, 16, False), (1024, 1408, 117, False), (1408, 1792, 24, True), (1792, T, 28, True)]
+            vT, 1, "v_pair1", 56, [(0, 1024, 131, False), (1024, 1408, 117, True), (1408, 1792, 28, True), (1792, T, 139, True)]
         )
+        nc.sync.dma_start(row_scale[:], us.rearrange("b (p t) o -> p b (t o)", t=PACK))
         labels = []
         for b in range(B):
             labels.append(placed("labels%d" % b, [P, PACK, N], 8 * b))
             nc.sync.dma_start(labels[b][:], y[b].rearrange("(p t) i -> p t i", t=PACK))
 
         heads = placed("heads", [P, 2 * B * K], 80, U32)
-        tails = placed("tails", [P, 3 * K], 88, U32)
+        tails = [placed("tails%d" % b, [P, 2 * K], kib, U32) for b, kib in enumerate((46, 141))]
         head_planes = heads[:].bitcast(BF16).rearrange("p (u b x) -> p b u x", u=2, b=B)
-        tail_planes = tails[:].bitcast(BF16).rearrange("p (u x) -> p u x", u=3)
+        tail_planes = [tile[:].bitcast(BF16).rearrange("p (u x) -> p u x", u=2) for tile in tails]
         gather(u_pair0, head_list, 0, B * K, heads[:, 0 : B * K])
         for dst, src in early_casts:
             nc.vector.tensor_copy(dst, src)
@@ -203,33 +211,36 @@ def tile_attend_gmf_nce_vu_kernel(tc, uT, vT, y, us, ts, offs, uoffs, out_0, out
         gather(u_pair1, head_list, 0, B * K, heads[:, B * K : 2 * B * K])
         for b in range(B):
             nc.vector.tensor_copy(slot_scale[b][:], banks[b][:, :, P - 1])
-        nc.vector.tensor_scalar(half_scale[:], row_scale[:, 0, :], 0.5, None, MULT)
         x = [held("x%d" % b, [P, K * PACK], BF16) for b in range(B)]
         w = [held("w0", [P, K * PACK], BF16)]
         for b in range(B):
             pack(x[b], head_planes[:, b], 0, P)
         for b in range(B):
             quantize(xq[b], x[b][:], E4M3)
-        gather(v_pair0, tail_list, 0, B * K, tails[:, 0 : B * K])
+        for b in range(B):
+            gather(v_pair0, tail_list, b * K, K, tails[b][:, 0:K])
 
-        x0_turned = placed("x0_turned", [P, K * PACK], 114, BF16)
-        turn(x0_turned, x[0], False, banks[3:5])
-        sc_a = placed("sc_a", [P, PACK, HALF], 119)
+        x0_turned = placed("x0_turned", [P, K * PACK], 131, BF16)
+        turn(x0_turned, x[0], banks[3:5])
+        sc_a = placed("sc_a", [P, PACK, HALF], 135)
         for j in range(2):
             nc.tensor.transpose(banks[2][:, j, :], slot_scale[0][:, j : j + 1].to_broadcast([P, P]), ident[:])
+        nc.scalar.activation(half_scale[:], row_scale[:, 0, :], COPY, scale=0.5)
         for t in range(PACK):
-            nc.scalar.activation(sc_a[:, t, :], flat(banks[2])[:, 0:HALF], COPY, scale=half_scale[:, t : t + 1])
+            nc.scalar.activation(
+                in_list_order(sc_a[:, t, :]), by_quad(flat(banks[2])[:, 0:HALF]), COPY, scale=half_scale[:, t : t + 1]
+            )
 
         for dst, src in late_casts:
             nc.vector.tensor_copy(dst, src)
         for half in range(2):
-            gather(v_pair1, tail_list, half * HALF, HALF, tails[:, 2 * K + half * HALF : 2 * K + (half + 1) * HALF])
+            gather(v_pair1, tail_list, half * HALF, HALF, tails[0][:, K + half * HALF : K + (half + 1) * HALF])
         for half in range(2):
-            pack(w[0], tail_planes[:, 0:3:2], half * QUADS, (half + 1) * QUADS)
+            pack(w[0], tail_planes[0], half * QUADS, (half + 1) * QUADS)
         for half in range(2):
             quantize_half(wq[0], w[0], E4M3, half)
 
-        logits = [placed("logits%d" % b, [P, PACK, R], 48) for b in range(B)]
+        logits = [placed("logits%d" % b, [P, PACK, R], 24) for b in range(B)]
         prob0 = placed("prob0", [P, PACK, N], 16)
         for c in range(2):
             rows = slice(c * HALF, (c + 1) * HALF)
@@ -258,44 +269,33 @@ def tile_attend_gmf_nce_vu_kernel(tc, uT, vT, y, us, ts, offs, uoffs, out_0, out
                 in_list_order(prob0[:, t, 0:HALF]), by_quad(flat(bank)[:, 0:HALF]), TANH, scale=half_scale[:, t : t + 1]
             )
         for j in range(2, 4):
-            scaled_logits(banks[j], 0, j)
+            scaled_logits(banks[j - 2], 0, j)
 
-        diff_a = placed("diff_a", [P, PACK, HALF], 94)
-        h0 = placed("h0", [P, K * PACK], 72, BF16)
-        for t in range(PACK):
-            nc.vector.scalar_tensor_tensor(
-                by_quad(diff_a[:, t, :]),
-                in_list_order(labels[0][:, t, 0:HALF]),
-                -2.0,
-                in_list_order(prob0[:, t, 0:HALF]),
-                MULT,
-                ADD,
-            )
-        nc.vector.scalar_tensor_tensor(
-            h0[:].rearrange("p (s q t) -> p s q t", s=PACK, t=PACK)[:, :, 0:QUADS, :],
-            diff_a[:].rearrange("p t (s q) -> p s q t", s=PACK),
-            1.0,
-            sc_a[:].rearrange("p t (s q) -> p s q t", s=PACK),
-            ADD,
-            MULT,
-        )
-        quantize_half(hr0, h0, E5M2, 0)
-
-        gather(v_pair1, tail_list, K, K, tails[:, 2 * K : 3 * K])
+        planes0 = placed("planes0", [P, PACK, N], 94, BF16)
+        quarters = [slice(c * P, (c + 1) * P) for c in range(PACK)]
+        h0_parts = [tail_planes[1][:, 1, 0:K], placed("h0_quarter1", [P, K], 88, BF16)[:]]
+        for t in range(0, PACK, 2):
+            part = prob0[:, t : t + 2, 0:HALF]
+            nc.vector.scalar_tensor_tensor(part, labels[0][:, t : t + 2, 0:HALF], -2.0, part, MULT, ADD)
+        for cols in quarters[0:2]:
+            nc.vector.scalar_tensor_tensor(planes0[:, :, cols], prob0[:, :, cols], 1.0, sc_a[:, :, cols], ADD, MULT)
+        for part, cols in zip(h0_parts, quarters):
+            nc.vector.tensor_copy(*interleaving(part, planes0, cols))
+        for part, cols in zip(h0_parts, quarters):
+            quantize_slots(hr0, part, cols)
         quantize(xr0, x0_turned[:], E4M3)
-        windows[1].append(placed("window1_2", [P, T], 56))
-        nc.vector.memset(windows[1][2][:], 0.0)
-        w.append(placed("w1", [P, K * PACK], 94, BF16))
-        pack(w[1], tail_planes[:, 1:3], 0, P)
-        quantize(wq[1], w[1][:], E4M3)
+        for t in range(2, PACK):
+            windows[1].append(placed("window1_%d" % t, [P, T], 24 + 8 * t))
+            nc.vector.memset(windows[1][t][:], 0.0)
+        gather(v_pair1, tail_list, K, K, tails[1][:, K : 2 * K])
 
-        half_stages = [held("half_stage%d" % j, [P, HALF]) for j in range(8)]
+        half_stages = [held("half_stage%d" % j, [P, HALF]) for j in range(7)]
         for t in range(2):
             tail_gradient(banks[4 + t], t, xr0, hr0, slice(0, HALF), 0, half_stages[t], False)
 
         diff_b = placed("diff_b", [P, PACK, HALF], 88)
         for t in range(PACK):
-            bank = banks[t // 2]
+            bank = banks[2 + t // 2]
             if t % 2 == 0:
                 for tt in range(2):
                     for j in range(2):
@@ -317,43 +317,47 @@ def tile_attend_gmf_nce_vu_kernel(tc, uT, vT, y, us, ts, offs, uoffs, out_0, out
             )
         for t in range(2, PACK):
             tail_gradient(banks[4 + t], t, xr0, hr0, slice(0, HALF), 0, half_stages[t], False)
+        h0_second = placed("h0_second", [P, HALF * PACK], 75, BF16)
         for c in range(2):
-            planes = placed("planes_b%d" % c, [P, PACK, P], 98 + c, BF16)
-            cols = slice(c * P, (c + 1) * P)
-            nc.gpsimd.tensor_tensor(planes[:], diff_b[:, :, cols], sc_b[:, :, cols], MULT)
-            quads = slice(QUADS + c * QUADS // 2, QUADS + (c + 1) * QUADS // 2)
-            nc.scalar.copy(dealt_slots(h0)[:, quads], by_slot(planes[:]))
-        quantize_half(hr0, h0, E5M2, 1)
+            cols, slots = quarters[c], quarters[2 + c]
+            nc.gpsimd.tensor_tensor(planes0[:, :, slots], diff_b[:, :, cols], sc_b[:, :, cols], MULT)
+            nc.scalar.copy(*interleaving(h0_second[:, c * K : (c + 1) * K], planes0, slots))
+        quantize_slots(hr0, h0_second[:], slice(HALF, K))
+        w.append(placed("w1", [P, K * PACK], 72, BF16))
+        pack(w[1], tail_planes[1], 0, P)
+        quantize(wq[1], w[1][:], E4M3)
 
-        w0_turned = placed("w0_turned", [P, K * PACK], 30, BF16)
-        turn(w0_turned, w[0], False, (banks[5], banks[4]))
-        wi0 = (placed("wi0_codes", [P, K], 99.5, U32), placed("wi0_scales", [P, K], 101.5, U8))
+        w0_turned = placed("w0_turned", [P, K * PACK], 117, BF16)
+        turn(w0_turned, w[0], (banks[5], banks[4]))
+        wi0 = (placed("wi0_codes", [P, K], 76, U32), placed("wi0_scales", [P, K], 78, U8))
         quantize(wi0, w0_turned[:], E4M3)
-        windows[1].append(placed("window1_3", [P, T], 24))
-        nc.gpsimd.memset(windows[1][3][:], 0.0)
+
+        for t in range(2):
+            tail_gradient(banks[2 + t], t, xr0, hr0, slice(HALF, K), HALF, half_stages[4 + t], False)
+        for t in range(2, PACK):
+            product(banks[3 - t], xr0, t, hr0, E5M2)
+        h0_turned = placed("h0_turned", [P, 2 * K], 86)
+        turn_planes(h0_turned, planes0, banks[2:4])
+        hi0 = wq[0]
+        quantize(hi0, h0_turned[:].bitcast(BF16), E5M2)
+        for t in range(2, PACK):
+            late_stage = placed("late_stage_b%d" % t, [P, HALF], 94 + t)
+            nc.scalar.copy(late_stage[:], flat(banks[3 - t])[:, HALF:K])
+            scatter(0, t, HALF, HALF, late_stage[:], False)
+
         slot_row = held("slot_row", [P, N])
         transposes(banks[7], lambda s: slot_scale[1][:, s : s + 1].to_broadcast([P, P]))
         nc.scalar.copy(in_list_order(slot_row[:]), by_quad(flat(banks[7])))
-        sc1 = placed("sc1", [P, PACK, N], 32)
+        sc1 = placed("sc1", [P, PACK, N], 88)
         for t in range(PACK):
             nc.gpsimd.tensor_scalar(sc1[:, t, :], slot_row[:], row_scale[:, 1, t : t + 1], 0.0, MULT, ADD)
-
-        for t, bank in enumerate((2, 3, 1)):
-            tail_gradient(banks[bank], t, xr0, hr0, slice(HALF, K), HALF, half_stages[4 + t], False)
-        product(banks[0], xr0, PACK - 1, hr0, E5M2)
-        h0_turned = placed("h0_turned", [P, K * PACK], 0, BF16)
-        turn(h0_turned, h0, True, banks[2:4])
-        hi0 = wq[0]
-        quantize(hi0, h0_turned[:], E5M2)
-        late_stage = placed("late_stage_b", [P, HALF], 72)
-        nc.scalar.copy(in_list_order(late_stage[:]), by_quad(flat(banks[0])[:, HALF:K]))
-        scatter(0, PACK - 1, HALF, HALF, late_stage[:], False)
 
         for s, bank in enumerate((6, 7, 4, 5)):
             scaled_logits(banks[bank], 1, s)
         prob1 = placed("prob1", [P, PACK, N], 16)
-        diff1 = placed("diff1", [P, PACK, N], 0)
-        stages = [held("stage%d" % j, [P, K]) for j in range(11)]
+        diff1 = placed("diff1", [P, PACK, N], 80)
+        stages = [held("stage%d" % j, [P, K]) for j in range(3)]
+        stages = stages + [placed("stage%d" % j, [P, K], 117 + 2 * j) for j in range(3, 11)]
         for t, bank in enumerate((6, 7, 4, 5)):
             transposes(banks[bank], lambda s: logits[1][:, s, t * P : (t + 1) * P])
             nc.scalar.activation(
@@ -362,45 +366,38 @@ def tile_attend_gmf_nce_vu_kernel(tc, uT, vT, y, us, ts, offs, uoffs, out_0, out
             nc.gpsimd.tensor_tensor(diff1[:, t, :], prob1[:, t, :], labels[1][:, t, :], SUBTRACT)
             if t == 1:
                 head_gradient(banks[1], 0, wi0, hi0, 0, stages[0], False)
-        head_gradient(banks[2], 1, wi0, hi0, 0, stages[1], False)
+        head_gradient(banks[7], 1, wi0, hi0, 0, stages[1], False)
 
-        head_gradient(banks[3], 2, wi0, hi0, 0, stages[2], False)
-        product(banks[0], wi0, PACK - 1, hi0, E5M2)
-        nc.scalar.copy(half_stages[7][:], flat(banks[0])[:, 0:HALF])
-        scatter(1, PACK - 1, 0, HALF, half_stages[7][:], False)
+        head_gradient(banks[4], 2, wi0, hi0, 0, stages[2], False)
+        product(banks[5], wi0, PACK - 1, hi0, E5M2)
+        nc.scalar.copy(half_stages[6][:], flat(banks[5])[:, 0:HALF])
+        scatter(1, PACK - 1, 0, HALF, half_stages[6][:], False)
 
-        x1_turned = placed("x1_turned", [P, K * PACK], 114, BF16)
-        turn(x1_turned, x[1], False, (banks[7], banks[4]))
-        w1_turned = placed("w1_turned", [P, K * PACK], 88, BF16)
-        turn(w1_turned, w[1], False, (banks[5], banks[1]))
-        h1 = placed("h1", [P, K * PACK], 119, BF16)
+        x1_turned = placed("x1_turned", [P, K * PACK], 24, BF16)
+        turn(x1_turned, x[1], banks[2:4])
+        w1_turned = placed("w1_turned", [P, K * PACK], 28, BF16)
+        turn(w1_turned, w[1], banks[6:8])
+        h1 = placed("h1", [P, K * PACK], 98, BF16)
         planes = placed("planes1", [P, PACK, N], 102, BF16)
         for c in range(PACK):
             cols = slice(c * P, (c + 1) * P)
             nc.gpsimd.tensor_tensor(planes[:, :, cols], diff1[:, :, cols], sc1[:, :, cols], MULT)
-            quads = slice(c * P // PACK, (c + 1) * P // PACK)
-            nc.scalar.copy(dealt_slots(h1)[:, quads], by_slot(planes[:])[:, quads])
-        xr1 = (placed("xr1_codes", [P, K], 0, U32), placed("xr1_scales", [P, K], 2, U8))
-        wi1 = (placed("wi1_codes", [P, K], 4, U32), placed("wi1_scales", [P, K], 6, U8))
+            nc.scalar.copy(*interleaving(h1[:, c * K : (c + 1) * K], planes, cols))
+        xr1 = (placed("xr1_codes", [P, K], 80, U32), placed("xr1_scales", [P, K], 82, U8))
+        wi1 = (placed("wi1_codes", [P, K], 84, U32), placed("wi1_scales", [P, K], 86, U8))
         hr1, hi1 = xq[1], wq[1]
         quantize(xr1, x1_turned[:], E4M3)
         quantize(wi1, w1_turned[:], E4M3)
         quantize(hr1, h1[:], E5M2)
-        late_stage = placed("late_stage_h", [P, HALF], 32)
-        nc.scalar.copy(late_stage[:], flat(banks[0])[:, HALF:K])
+        late_stage = placed("late_stage_h", [P, HALF], 90)
+        nc.scalar.copy(late_stage[:], flat(banks[5])[:, HALF:K])
         scatter(1, PACK - 1, HALF, HALF, late_stage[:], False)
 
-        for t, bank in enumerate((2, 3, 6, 7)):
+        for t, bank in enumerate((2, 3, 1, 0)):
             tail_gradient(banks[bank], t, xr1, hr1, slice(0, K), K, stages[3 + t], True)
             if t == 1:
-                h1_turned = placed("h1_turned", [P, 2 * K], 80)
-                words = planes[:].rearrange("p t i -> p (t i)").bitcast(F32).rearrange("p (t q u) -> p t u q", t=PACK, u=2)
-                for j in range(2):
-                    transposes(banks[4 + j], lambda a: words[:, 2 * j + a // 2, a % 2, :])
-                    nc.scalar.copy(
-                        h1_turned[:].rearrange("q (p j a) -> q j p a", j=2, a=PACK)[:, j],
-                        banks[4 + j][:].rearrange("q a p -> q p a"),
-                    )
+                h1_turned = placed("h1_turned", [P, 2 * K], 0)
+                turn_planes(h1_turned, planes, (banks[4], banks[6]))
                 quantize(hi1, h1_turned[:].bitcast(BF16), E5M2)
-        for t, bank in enumerate((1, 0, 2, 3)):
+        for t, bank in enumerate((7, 5, 2, 3)):
             head_gradient(banks[bank], t, wi1, hi1, K, stages[7 + t], True)

@@ -15,17 +15,14 @@ E4M3 = mybir.dt.float8_e4m3fn_x4
 E5M2 = mybir.dt.float8_e5m2_x4
 MULT = mybir.AluOpType.mult
 ADD = mybir.AluOpType.add
-SUBTRACT = mybir.AluOpType.subtract
 COPY = mybir.ActivationFunctionType.Copy
-SIGMOID = mybir.ActivationFunctionType.Sigmoid
 TANH = mybir.ActivationFunctionType.Tanh
 
 P = 128
 PACK = 4
 K = P * PACK
-HALF = K // 2
-QUADS = HALF // PACK
-LIST_COLS = K // 16
+LISTED = B * K
+PIECE = 256
 KIB = 1024
 
 
@@ -44,57 +41,34 @@ def tile_attend_gmf_nce_vu_kernel(tc, uT, vT, y, us, ts, offs, uoffs, out_0, out
         def placed(name, shape, kib, dtype=F32):
             return shared.tile(shape, dtype, name=name, align_bytes=64, offset=int(kib * KIB))
 
+        def operand(name, columns):
+            return held(name + "_codes", [P, columns], U32), held(name + "_scales", [P, columns], U8)
+
         def flat(bank):
             return bank[:].rearrange("p s q -> p (s q)")
 
-        head_list = keep.tile([P, B * LIST_COLS], U16, name="head_list")
-        tail_list = keep.tile([P, B * LIST_COLS], U16, name="tail_list")
+        head_list = keep.tile([P, LISTED // 16], U16, name="head_list")
+        tail_list = keep.tile([P, LISTED // 16], U16, name="tail_list")
         row_scale = held("row_scale", [P, B, PACK])
-        half_scale = held("half_scale", [P, PACK])
-        slot_scale = [held("slot_scale%d" % b, [P, PACK]) for b in range(B)]
+        half_scale = held("half_scale", [P, B, PACK])
+        slot_scale = held("slot_scale", [P, B, PACK])
         ident = held("ident", [P, P])
-        operands = [(held("codes%d" % j, [P, K], U32), held("scales%d" % j, [P, K], U8)) for j in range(6)]
-        xq, wq, xr0, hr0 = operands[0:2], operands[2:4], operands[4], operands[5]
         make_identity(nc, ident[:])
 
         def entries(lst, first, count):
             return lst[:, first // 16 : (first + count) // 16]
 
-        def load_pair(table, u, name, kib, cuts):
-            rows = table.rearrange("(p u e) c -> p u e c", u=2, e=2)
-            pair = placed(name, [P, T, 2], kib, BF16)
-            late = []
-            for c0, c1, raw_kib, on_vector in cuts:
-                raw = placed("%s_raw%d" % (name, c0), [P, 2, c1 - c0], raw_kib)
-                nc.sync.dma_start(raw[:], rows[:, u, :, c0:c1])
-                src = raw[:].rearrange("p e c -> p c e")
-                if on_vector:
-                    late.append((pair[:, c0:c1, :], src))
-                else:
-                    nc.scalar.activation(pair[:, c0:c1, :], src, COPY)
-            return pair, late
+        def gather(on_vector, dst, table, lst, first, count):
+            src = table[:].indirect(entries(lst, first, count))
+            if on_vector:
+                nc.vector.tensor_copy(dst, src)
+            else:
+                nc.scalar.activation(dst, src, COPY)
 
-        def gather(pair, lst, first, count, dst):
-            window = pair[:].rearrange("p c e -> p (c e)").bitcast(U32)
-            nc.vector.tensor_copy(dst, window.indirect(entries(lst, first, count)))
+        def quantize(op, src, fmt):
+            nc.vector.quantize_mx(op[0][:].bitcast(fmt), op[1][:], src)
 
-        def pack(dst, planes, q0, q1):
-            nc.vector.tensor_copy(
-                dst[:].rearrange("p (s q u e) -> p q s u e", s=PACK, u=2, e=2)[:, q0:q1],
-                planes.rearrange("p u (q s e) -> p q s u e", s=PACK, e=2)[:, q0:q1],
-            )
-
-        def quantize(operand, src, fmt):
-            nc.vector.quantize_mx(operand[0][:].bitcast(fmt), operand[1][:], src)
-
-        def quantize_half(operand, src, fmt, half):
-            for s in range(PACK):
-                cols = slice((half * PACK + s) * QUADS, (half * PACK + s + 1) * QUADS)
-                first = s * K + half * HALF
-                nc.vector.quantize_mx(operand[0][:, cols].bitcast(fmt), operand[1][:, cols], src[:, first : first + HALF])
-
-        def product(bank, stationary, t, moving, moving_fmt):
-            cols = slice(t * P, (t + 1) * P)
+        def product(bank, stationary, cols, moving, moving_fmt):
             nc.tensor.matmul_mx(
                 flat(bank),
                 lhsT=stationary[0][:, cols].bitcast(E4M3),
@@ -109,295 +83,218 @@ def tile_attend_gmf_nce_vu_kernel(tc, uT, vT, y, us, ts, offs, uoffs, out_0, out
             for s in range(PACK):
                 nc.tensor.transpose(bank[:, s, :], source(s), ident[:])
 
-        def turn(dst, tile, two_banks):
-            words = tile[:].bitcast(F32).rearrange("p (s q u) -> p u s q", s=PACK, u=2)
-            for u, bank in enumerate(two_banks):
-                transposes(bank, lambda s: words[:, u, s, :])
-                halves = flat(bank).bitcast(BF16)
-                src = halves.rearrange("q (s p e) -> q e p s", s=PACK, e=2)
-                out = dst[:].rearrange("q (u e p s) -> q u e p s", u=2, e=2, s=PACK)[:, u]
-                nc.scalar.copy(out, src)
+        def block(j):
+            return slice(j * P, (j + 1) * P)
 
-        def in_list_order(dst):
-            return dst.rearrange("p (q s) -> p q s", s=PACK)
+        def copy(on_vector, dst, src):
+            if on_vector:
+                nc.vector.tensor_copy(dst, src)
+            else:
+                nc.scalar.copy(dst, src)
 
-        def by_quad(dealt):
-            return dealt.rearrange("p (s q) -> p q s", s=PACK)
+        def turn_plane(on_vector, dst, plane, bank):
+            words = plane.bitcast(F32).rearrange("p (b q u) -> p b u q", b=B, u=2)
+            transposes(bank, lambda a: words[:, a // 2, a % 2, :])
+            copy(on_vector, dst.rearrange("q (b p u) -> q b p u", b=B, u=2), bank[:].rearrange("q (b u) p -> q b p u", u=2))
 
-        def scaled_logits(bank, b, j):
-            product(bank, wq[b], j, xq[b], E4M3)
-            nc.scalar.activation(logits[b][:, j, :], flat(bank), COPY, scale=slot_scale[b][:, j : j + 1])
-
-        def interleaving(h, planes, cols):
-            quads = slice(cols.start // PACK, cols.stop // PACK)
-            return (
-                h.rearrange("p (q s t) -> p q t s", s=PACK, t=PACK),
-                planes[:].rearrange("p t (q s) -> p q t s", s=PACK)[:, quads],
+        def interleave(dst, planes):
+            nc.vector.tensor_copy(
+                dst[:].rearrange("p (q s t) -> p q t s", s=PACK, t=PACK), planes.rearrange("p t (q s) -> p q t s", s=PACK)
             )
 
-        def quantize_slots(operand, h, cols):
-            nc.vector.quantize_mx(operand[0][:, cols].bitcast(E5M2), operand[1][:, cols], h)
+        tail_scale_row = placed("tail_scale_row", [P, T], 64)
+        nc.sync.dma_start(tail_scale_row[P - 1 : P, :], ts[0:1, :])
+        nc.sync.dma_start(tail_list[:], offs)
+        tables = []
+        for side, table in enumerate((uT, vT)):
+            rows = table.rearrange("(p t) c -> p t c", t=PACK)
+            tables.append([])
+            for t in range(PACK):
+                tables[side].append(placed("table%d_%d" % (side, t), [P, T], 32 * side + 8 * t))
+                nc.sync.dma_start(tables[side][t][:], rows[:, t, :])
+                if side == 0 and t == 0:
+                    nc.sync.dma_start(head_list[:], uoffs)
+                    nc.sync.dma_start(row_scale[:], us.rearrange("b (p t) o -> p b (t o)", t=PACK))
 
-        def turn_planes(dst, planes, two_banks):
-            words = planes[:].rearrange("p t i -> p (t i)").bitcast(F32).rearrange("p (t q u) -> p t u q", t=PACK, u=2)
+        nc.vector.memset(tail_scale_row[0 : P - 1, :], 0.0)
+        windows = [held("window%d" % j, [P, T]) for j in range(5)]
+        for window in windows[0:2]:
+            nc.vector.memset(window[:], 0.0)
+        for window in windows[2:]:
+            nc.gpsimd.memset(window[:], 0.0)
+
+        picked = placed("picked", [P, LISTED], 80)
+        gather(True, picked[:], tail_scale_row, tail_list, 0, LISTED)
+        labels = []
+        for b in range(B):
+            labels.append(placed("labels%d" % b, [P, PACK, N], 64 + 8 * b))
+            nc.sync.dma_start(labels[b][:], y[b].rearrange("(p t) i -> p t i", t=PACK))
+        for b in range(B):
+            transposes(banks[b], lambda j: picked[:, b * N + j * P : b * N + (j + 1) * P])
+            nc.vector.tensor_copy(slot_scale[:, b, :], banks[b][:, :, P - 1])
+        nc.gpsimd.tensor_scalar(half_scale[:], row_scale[:], 0.5, 0.0, MULT, ADD)
+        slot_row = placed("slot_row", [P, LISTED], 84)
+        half_sc = []
+        for b in range(B):
+            transposes(banks[2 + b], lambda j: slot_scale[:, b, j : j + 1].to_broadcast([P, P]))
+            nc.vector.tensor_copy(slot_row[:, b * N : (b + 1) * N], flat(banks[2 + b]))
+            half_sc.append(placed("half_sc%d" % b, [P, PACK, N], 88 + 8 * b))
+            for t in range(PACK):
+                nc.gpsimd.tensor_scalar(
+                    half_sc[b][:, t, :], slot_row[:, b * N : (b + 1) * N], half_scale[:, b, t : t + 1], 0.0, MULT, ADD
+                )
+
+        x_planes = placed("x_planes", [P, PACK * LISTED], 104, BF16)
+        w_planes = placed("w_planes", [P, PACK * LISTED], 112, BF16)
+        xq = [operand("xq%d" % b, K) for b in range(B)]
+        wq = [operand("wq%d" % b, K) for b in range(B)]
+        xr = [operand("xr%d" % t, B * P) for t in range(PACK)]
+        wi = [operand("wi%d" % t, B * P) for t in range(2)]
+        wi_late = operand("wi_late", 2 * B * P)
+        for t in range(2):
+            cols = slice(t * B * P, (t + 1) * B * P)
+            wi.append((wi_late[0][:, cols], wi_late[1][:, cols]))
+
+        def plane(planes, t):
+            return planes[:, t * LISTED : (t + 1) * LISTED]
+
+        def group_planes(planes, b):
+            return planes[:].rearrange("p (t b i) -> p b t i", t=PACK, b=B)[:, b]
+
+        x_turned = []
+        for t in range(PACK):
+            gather(t == 2, plane(x_planes, t), tables[0][t], head_list, 0, LISTED)
+            x_turned.append(placed("x_turned%d" % t, [P, K], 120 + 2 * t))
+            turn_plane(True, x_turned[t][:], plane(x_planes, t), banks[4 + t])
+        x = [placed("x%d" % b, [P, K * PACK], 136 + 4 * b, BF16) for b in range(B)]
+        for b in range(B):
+            nc.vector.tensor_copy(
+                x[b][:].rearrange("p (s q t) -> p q s t", s=PACK, t=PACK),
+                group_planes(x_planes, b).rearrange("p t (q s) -> p q s t", s=PACK),
+            )
+        for t in range(PACK):
+            quantize(xr[t], x_turned[t][:].bitcast(BF16), E4M3)
+        for b in range(B):
+            quantize(xq[b], x[b][:], E4M3)
+
+        w_turned = [placed("w_turned%d" % t, [P, K], 128 + 2 * t) for t in range(2)]
+        for t in range(PACK - 1):
+            gather(False, plane(w_planes, t), tables[1][t], tail_list, 0, LISTED)
+            if t < 2:
+                turn_plane(True, w_turned[t][:], plane(w_planes, t), banks[4 + t])
+                quantize(wi[t], w_turned[t][:].bitcast(BF16), E4M3)
+        last = PACK - 1
+        for b in range(B):
+            gather(b == 0, plane(w_planes, last)[:, b * N : (b + 1) * N], tables[1][last], tail_list, b * N, N)
+        w = [placed("w%d" % b, [P, K * PACK], 144 + 4 * b, BF16) for b in range(B)]
+        interleave(w[0], group_planes(w_planes, 0))
+        quantize(wq[0], w[0][:], E4M3)
+        w_late = placed("w_late", [P, 2 * K], 56)
+        for t in range(2):
+            turn_plane(False, w_late[:, t * K : (t + 1) * K], plane(w_planes, 2 + t), banks[6 + t])
+        interleave(w[1], group_planes(w_planes, 1))
+        quantize(wi_late, w_late[:].bitcast(BF16), E4M3)
+        quantize(wq[1], w[1][:], E4M3)
+
+        logits = placed("logits", [P, PACK, R], 152)
+        prob = [placed("prob%d" % b, [P, PACK, N], 160 + 8 * b) for b in range(B)]
+        h_planes = [placed("h_planes%d" % b, [P, PACK * N], 104 + 4 * b, BF16) for b in range(B)]
+        h = [placed("h%d" % b, [P, K * PACK], 136 + 4 * b, BF16) for b in range(B)]
+        h_turned = [placed("h_turned%d" % b, [P, 2 * K], 120 + 4 * b) for b in range(B)]
+        hr, hi = xq, wq
+        stages = [[placed("stage%d_%d" % (o, t), [P, LISTED], 32 + 16 * o + 4 * t) for t in range(PACK)] for o in range(2)]
+
+        def scores(b, first_banks, second_banks):
+            for j, bank in enumerate(first_banks):
+                product(bank, wq[b], block(j), xq[b], E4M3)
+                nc.scalar.activation(logits[:, j, :], flat(bank), COPY, scale=slot_scale[:, b, j : j + 1])
+            for t, bank in enumerate(second_banks):
+                transposes(bank, lambda j: logits[:, j, block(t)])
+                nc.scalar.activation(prob[b][:, t, :], flat(bank), TANH, scale=half_scale[:, b, t : t + 1])
+
+        def weights(b):
+            planes = h_planes[b][:].rearrange("p (t i) -> p t i", t=PACK)
+            for t in range(PACK + 1):
+                if t < PACK:
+                    part = prob[b][:, t, :]
+                    nc.vector.scalar_tensor_tensor(part, labels[b][:, t, :], -2.0, part, MULT, ADD)
+                if t > 0:
+                    nc.vector.scalar_tensor_tensor(
+                        planes[:, t - 1, :], prob[b][:, t - 1, :], 1.0, half_sc[b][:, t - 1, :], ADD, MULT
+                    )
+            interleave(h[b], planes)
+            quantize(hr[b], h[b][:], E5M2)
+
+        def turn_weights(b, two_banks):
+            words = h_planes[b][:].bitcast(F32).rearrange("p (t q u) -> p t u q", t=PACK, u=2)
             for j, bank in enumerate(two_banks):
                 transposes(bank, lambda a: words[:, 2 * j + a // 2, a % 2, :])
                 nc.scalar.copy(
-                    dst[:].rearrange("q (p j a) -> q j p a", j=2, a=PACK)[:, j], bank[:].rearrange("q a p -> q p a")
+                    h_turned[b][:].rearrange("q (p j a) -> q j p a", j=2, a=PACK)[:, j], bank[:].rearrange("q a p -> q p a")
                 )
 
-        def scatter(o, t, first, count, staged, last):
-            out, lst = sides[o]
-            nc.vector.tensor_copy(windows[o][t][:].indirect(entries(lst, first, count)), staged)
-            if last:
-                nc.sync.dma_start(out.rearrange("(p t) c -> p t c", t=PACK)[:, t, :], windows[o][t][:])
+        def gradient(o, b, t, bank, on_vector):
+            product(bank, (xr, wi)[o][t], block(b), (hr, hi)[o][b], E5M2)
+            copy(on_vector, stages[o][t][:, b * K : (b + 1) * K], flat(bank))
 
-        def tail_gradient(bank, t, xr, hr, cols, first, staged, last):
-            product(bank, xr, t, hr, E5M2)
-            nc.scalar.copy(staged[:], flat(bank)[:, cols])
-            scatter(0, t, first, cols.stop - cols.start, staged[:], last)
+        def store(out, t, window):
+            nc.sync.dma_start(out.rearrange("(p t) c -> p t c", t=PACK)[:, t, :], window[:])
 
-        def head_gradient(bank, t, wi, hi, first, staged, last):
-            product(bank, wi, t, hi, E5M2)
-            nc.scalar.copy(staged[:], flat(bank))
-            scatter(1, t, first, K, staged[:], last)
-
-        sides = ((out_0, tail_list), (out_1, head_list))
-        tail_scale_row = placed("tail_scale_row", [P, T], 98)
-        nc.sync.dma_start(tail_scale_row[P - 1 : P, :], ts[0:1, :])
-        nc.sync.dma_start(tail_list[:], offs)
-        nc.vector.memset(tail_scale_row[0 : P - 1, :], 0.0)
-        windows = [[held("window0_%d" % t, [P, T]) for t in range(PACK)], []]
-        nc.vector.memset(windows[0][0][:], 0.0)
-        picked = placed("picked", [P, B * N], 72)
-        dealt = placed("dealt", [P, N], 76)
-        nc.vector.tensor_copy(picked[:], tail_scale_row[:].indirect(tail_list[:]))
-        nc.vector.tensor_copy(
-            dealt[:].rearrange("p (h s q) -> p h s q", h=2, s=PACK),
-            picked[:, 0:N].rearrange("p (h q s) -> p h s q", h=2, s=PACK),
-        )
-        transposes(banks[0], lambda j: dealt[:, j * P : (j + 1) * P])
-        transposes(banks[1], lambda s: picked[:, N : 2 * N].rearrange("p (q s) -> p s q", s=PACK)[:, s, :])
-        for window in windows[0][1:]:
-            nc.vector.memset(window[:], 0.0)
-        nc.vector.memset(hr0[0][:, HALF:K], 0)
-        nc.vector.memset(hr0[1][:, HALF:K], 0)
-
-        u_pair0, unused = load_pair(uT, 0, "u_pair0", 40, [(0, T // 2, 0, False), (T // 2, T, 64, False)])
-        nc.sync.dma_start(head_list[:], uoffs)
-        u_pair1, early_casts = load_pair(
-            uT, 1, "u_pair1", 48, [(0, 1024, 8, False), (1024, 1536, 24, False), (1536, T, 106, True)]
-        )
-        v_pair0, unused = load_pair(vT, 0, "v_pair0", 32, [(0, T // 2, 16, False), (T // 2, T, 123, False)])
-        v_pair1, late_casts = load_pair(
-            vT, 1, "v_pair1", 56, [(0, 1024, 131, False), (1024, 1408, 117, True), (1408, 1792, 28, True), (1792, T, 139, True)]
-        )
-        nc.sync.dma_start(row_scale[:], us.rearrange("b (p t) o -> p b (t o)", t=PACK))
-        labels = []
-        for b in range(B):
-            labels.append(placed("labels%d" % b, [P, PACK, N], 8 * b))
-            nc.sync.dma_start(labels[b][:], y[b].rearrange("(p t) i -> p t i", t=PACK))
-
-        heads = placed("heads", [P, 2 * B * K], 80, U32)
-        tails = [placed("tails%d" % b, [P, 2 * K], kib, U32) for b, kib in enumerate((46, 141))]
-        head_planes = heads[:].bitcast(BF16).rearrange("p (u b x) -> p b u x", u=2, b=B)
-        tail_planes = [tile[:].bitcast(BF16).rearrange("p (u x) -> p u x", u=2) for tile in tails]
-        gather(u_pair0, head_list, 0, B * K, heads[:, 0 : B * K])
-        for dst, src in early_casts:
-            nc.vector.tensor_copy(dst, src)
-        for t, kib in enumerate((64, 106)):
-            windows[1].append(placed("window1_%d" % t, [P, T], kib))
-            nc.gpsimd.memset(windows[1][t][:], 0.0)
-        gather(u_pair1, head_list, 0, B * K, heads[:, B * K : 2 * B * K])
-        for b in range(B):
-            nc.vector.tensor_copy(slot_scale[b][:], banks[b][:, :, P - 1])
-        x = [held("x%d" % b, [P, K * PACK], BF16) for b in range(B)]
-        w = [held("w0", [P, K * PACK], BF16)]
-        for b in range(B):
-            pack(x[b], head_planes[:, b], 0, P)
-        for b in range(B):
-            quantize(xq[b], x[b][:], E4M3)
-        for b in range(B):
-            gather(v_pair0, tail_list, b * K, K, tails[b][:, 0:K])
-
-        x0_turned = placed("x0_turned", [P, K * PACK], 131, BF16)
-        turn(x0_turned, x[0], banks[3:5])
-        sc_a = placed("sc_a", [P, PACK, HALF], 135)
-        for j in range(2):
-            nc.tensor.transpose(banks[2][:, j, :], slot_scale[0][:, j : j + 1].to_broadcast([P, P]), ident[:])
-        nc.scalar.activation(half_scale[:], row_scale[:, 0, :], COPY, scale=0.5)
-        for t in range(PACK):
+        def tail_piece(t, c):
+            window = windows[t % 3]
+            first = c * PIECE
             nc.scalar.activation(
-                in_list_order(sc_a[:, t, :]), by_quad(flat(banks[2])[:, 0:HALF]), COPY, scale=half_scale[:, t : t + 1]
+                window[:].indirect(entries(tail_list, first, PIECE)), stages[0][t][:, first : first + PIECE], COPY
             )
+            if c == PACK - 1:
+                store(out_0, t, window)
 
-        for dst, src in late_casts:
-            nc.vector.tensor_copy(dst, src)
-        for half in range(2):
-            gather(v_pair1, tail_list, half * HALF, HALF, tails[0][:, K + half * HALF : K + (half + 1) * HALF])
-        for half in range(2):
-            pack(w[0], tail_planes[0], half * QUADS, (half + 1) * QUADS)
-        for half in range(2):
-            quantize_half(wq[0], w[0], E4M3, half)
+        def head_block(t):
+            window = windows[3 + t % 2]
+            nc.vector.tensor_copy(window[:].indirect(head_list[:]), stages[1][t][:])
+            store(out_1, t, window)
 
-        logits = [placed("logits%d" % b, [P, PACK, R], 24) for b in range(B)]
-        prob0 = placed("prob0", [P, PACK, N], 16)
-        for c in range(2):
-            rows = slice(c * HALF, (c + 1) * HALF)
-            for j in range(2):
-                nc.tensor.matmul_mx(
-                    flat(banks[c])[:, j * HALF : (j + 1) * HALF],
-                    lhsT=wq[0][0][:, j * P : (j + 1) * P].bitcast(E4M3),
-                    lhsT_scale=wq[0][1][:, j * P : (j + 1) * P],
-                    rhs=xq[0][0][:, rows].bitcast(E4M3),
-                    rhs_scale=xq[0][1][:, rows],
-                    start=True,
-                    stop=True,
-                )
-            for j in range(2):
-                nc.scalar.activation(
-                    logits[0][:, j, rows],
-                    flat(banks[c])[:, j * HALF : (j + 1) * HALF],
-                    COPY,
-                    scale=slot_scale[0][:, j : j + 1],
-                )
-        for t in range(PACK):
-            bank = banks[4 + t]
-            for j in range(2):
-                nc.tensor.transpose(bank[:, j, :], logits[0][:, j, t * P : (t + 1) * P], ident[:])
-            nc.scalar.activation(
-                in_list_order(prob0[:, t, 0:HALF]), by_quad(flat(bank)[:, 0:HALF]), TANH, scale=half_scale[:, t : t + 1]
-            )
-        for j in range(2, 4):
-            scaled_logits(banks[j - 2], 0, j)
-
-        planes0 = placed("planes0", [P, PACK, N], 94, BF16)
-        quarters = [slice(c * P, (c + 1) * P) for c in range(PACK)]
-        h0_parts = [tail_planes[1][:, 1, 0:K], placed("h0_quarter1", [P, K], 88, BF16)[:]]
-        for t in range(0, PACK, 2):
-            part = prob0[:, t : t + 2, 0:HALF]
-            nc.vector.scalar_tensor_tensor(part, labels[0][:, t : t + 2, 0:HALF], -2.0, part, MULT, ADD)
-        for cols in quarters[0:2]:
-            nc.vector.scalar_tensor_tensor(planes0[:, :, cols], prob0[:, :, cols], 1.0, sc_a[:, :, cols], ADD, MULT)
-        for part, cols in zip(h0_parts, quarters):
-            nc.vector.tensor_copy(*interleaving(part, planes0, cols))
-        for part, cols in zip(h0_parts, quarters):
-            quantize_slots(hr0, part, cols)
-        quantize(xr0, x0_turned[:], E4M3)
-        for t in range(2, PACK):
-            windows[1].append(placed("window1_%d" % t, [P, T], 24 + 8 * t))
-            nc.vector.memset(windows[1][t][:], 0.0)
-        gather(v_pair1, tail_list, K, K, tails[1][:, K : 2 * K])
-
-        half_stages = [held("half_stage%d" % j, [P, HALF]) for j in range(7)]
-        for t in range(2):
-            tail_gradient(banks[4 + t], t, xr0, hr0, slice(0, HALF), 0, half_stages[t], False)
-
-        diff_b = placed("diff_b", [P, PACK, HALF], 88)
-        for t in range(PACK):
-            bank = banks[2 + t // 2]
-            if t % 2 == 0:
-                for tt in range(2):
-                    for j in range(2):
-                        cols = slice((t + tt) * P, (t + tt + 1) * P)
-                        nc.tensor.transpose(bank[:, 2 * tt + j, :], logits[0][:, 2 + j, cols], ident[:])
-            nc.scalar.activation(
-                in_list_order(prob0[:, t, HALF:K]),
-                by_quad(flat(bank)[:, (t % 2) * HALF : (t % 2 + 1) * HALF]),
-                SIGMOID,
-                scale=row_scale[:, 0, t : t + 1],
-            )
-            nc.gpsimd.tensor_tensor(diff_b[:, t, :], prob0[:, t, HALF:K], labels[0][:, t, HALF:K], SUBTRACT)
-        sc_b = placed("sc_b", [P, PACK, HALF], 102)
-        for j in range(2):
-            nc.tensor.transpose(banks[4][:, j, :], slot_scale[0][:, 2 + j : 3 + j].to_broadcast([P, P]), ident[:])
-        for t in range(PACK):
-            nc.scalar.activation(
-                in_list_order(sc_b[:, t, :]), by_quad(flat(banks[4])[:, 0:HALF]), COPY, scale=row_scale[:, 0, t : t + 1]
-            )
-        for t in range(2, PACK):
-            tail_gradient(banks[4 + t], t, xr0, hr0, slice(0, HALF), 0, half_stages[t], False)
-        h0_second = placed("h0_second", [P, HALF * PACK], 75, BF16)
-        for c in range(2):
-            cols, slots = quarters[c], quarters[2 + c]
-            nc.gpsimd.tensor_tensor(planes0[:, :, slots], diff_b[:, :, cols], sc_b[:, :, cols], MULT)
-            nc.scalar.copy(*interleaving(h0_second[:, c * K : (c + 1) * K], planes0, slots))
-        quantize_slots(hr0, h0_second[:], slice(HALF, K))
-        w.append(placed("w1", [P, K * PACK], 72, BF16))
-        pack(w[1], tail_planes[1], 0, P)
-        quantize(wq[1], w[1][:], E4M3)
-
-        w0_turned = placed("w0_turned", [P, K * PACK], 117, BF16)
-        turn(w0_turned, w[0], (banks[5], banks[4]))
-        wi0 = (placed("wi0_codes", [P, K], 76, U32), placed("wi0_scales", [P, K], 78, U8))
-        quantize(wi0, w0_turned[:], E4M3)
-
-        for t in range(2):
-            tail_gradient(banks[2 + t], t, xr0, hr0, slice(HALF, K), HALF, half_stages[4 + t], False)
-        for t in range(2, PACK):
-            product(banks[3 - t], xr0, t, hr0, E5M2)
-        h0_turned = placed("h0_turned", [P, 2 * K], 86)
-        turn_planes(h0_turned, planes0, banks[2:4])
-        hi0 = wq[0]
-        quantize(hi0, h0_turned[:].bitcast(BF16), E5M2)
-        for t in range(2, PACK):
-            late_stage = placed("late_stage_b%d" % t, [P, HALF], 94 + t)
-            nc.scalar.copy(late_stage[:], flat(banks[3 - t])[:, HALF:K])
-            scatter(0, t, HALF, HALF, late_stage[:], False)
-
-        slot_row = held("slot_row", [P, N])
-        transposes(banks[7], lambda s: slot_scale[1][:, s : s + 1].to_broadcast([P, P]))
-        nc.scalar.copy(in_list_order(slot_row[:]), by_quad(flat(banks[7])))
-        sc1 = placed("sc1", [P, PACK, N], 88)
-        for t in range(PACK):
-            nc.gpsimd.tensor_scalar(sc1[:, t, :], slot_row[:], row_scale[:, 1, t : t + 1], 0.0, MULT, ADD)
-
-        for s, bank in enumerate((6, 7, 4, 5)):
-            scaled_logits(banks[bank], 1, s)
-        prob1 = placed("prob1", [P, PACK, N], 16)
-        diff1 = placed("diff1", [P, PACK, N], 80)
-        stages = [held("stage%d" % j, [P, K]) for j in range(3)]
-        stages = stages + [placed("stage%d" % j, [P, K], 117 + 2 * j) for j in range(3, 11)]
-        for t, bank in enumerate((6, 7, 4, 5)):
-            transposes(banks[bank], lambda s: logits[1][:, s, t * P : (t + 1) * P])
-            nc.scalar.activation(
-                in_list_order(prob1[:, t, :]), by_quad(flat(banks[bank])), SIGMOID, scale=row_scale[:, 1, t : t + 1]
-            )
-            nc.gpsimd.tensor_tensor(diff1[:, t, :], prob1[:, t, :], labels[1][:, t, :], SUBTRACT)
-            if t == 1:
-                head_gradient(banks[1], 0, wi0, hi0, 0, stages[0], False)
-        head_gradient(banks[7], 1, wi0, hi0, 0, stages[1], False)
-
-        head_gradient(banks[4], 2, wi0, hi0, 0, stages[2], False)
-        product(banks[5], wi0, PACK - 1, hi0, E5M2)
-        nc.scalar.copy(half_stages[6][:], flat(banks[5])[:, 0:HALF])
-        scatter(1, PACK - 1, 0, HALF, half_stages[6][:], False)
-
-        x1_turned = placed("x1_turned", [P, K * PACK], 24, BF16)
-        turn(x1_turned, x[1], banks[2:4])
-        w1_turned = placed("w1_turned", [P, K * PACK], 28, BF16)
-        turn(w1_turned, w[1], banks[6:8])
-        h1 = placed("h1", [P, K * PACK], 98, BF16)
-        planes = placed("planes1", [P, PACK, N], 102, BF16)
-        for c in range(PACK):
-            cols = slice(c * P, (c + 1) * P)
-            nc.gpsimd.tensor_tensor(planes[:, :, cols], diff1[:, :, cols], sc1[:, :, cols], MULT)
-            nc.scalar.copy(*interleaving(h1[:, c * K : (c + 1) * K], planes, cols))
-        xr1 = (placed("xr1_codes", [P, K], 80, U32), placed("xr1_scales", [P, K], 82, U8))
-        wi1 = (placed("wi1_codes", [P, K], 84, U32), placed("wi1_scales", [P, K], 86, U8))
-        hr1, hi1 = xq[1], wq[1]
-        quantize(xr1, x1_turned[:], E4M3)
-        quantize(wi1, w1_turned[:], E4M3)
-        quantize(hr1, h1[:], E5M2)
-        late_stage = placed("late_stage_h", [P, HALF], 90)
-        nc.scalar.copy(late_stage[:], flat(banks[5])[:, HALF:K])
-        scatter(1, PACK - 1, HALF, HALF, late_stage[:], False)
-
-        for t, bank in enumerate((2, 3, 1, 0)):
-            tail_gradient(banks[bank], t, xr1, hr1, slice(0, K), K, stages[3 + t], True)
-            if t == 1:
-                h1_turned = placed("h1_turned", [P, 2 * K], 0)
-                turn_planes(h1_turned, planes, (banks[4], banks[6]))
-                quantize(hi1, h1_turned[:].bitcast(BF16), E5M2)
-        for t, bank in enumerate((7, 5, 2, 3)):
-            head_gradient(banks[bank], t, wi1, hi1, K, stages[7 + t], True)
+        scores(0, banks[0:4], banks[4:8])
+        weights(0)
+        scores(1, banks[4:8], banks[0:4])
+        turn_weights(0, banks[4:6])
+        gradient(0, 0, 0, banks[6], False)
+        tail_piece(0, 0)
+        tail_piece(0, 1)
+        weights(1)
+        quantize(hi[0], h_turned[0][:].bitcast(BF16), E5M2)
+        turn_weights(1, banks[4:6])
+        gradient(1, 0, 0, banks[7], True)
+        quantize(hi[1], h_turned[1][:].bitcast(BF16), E5M2)
+        gradient(0, 0, 1, banks[4], False)
+        tail_piece(1, 0)
+        gradient(1, 1, 0, banks[0], True)
+        head_block(0)
+        gradient(0, 1, 0, banks[5], False)
+        tail_piece(1, 1)
+        tail_piece(0, 2)
+        gradient(1, 0, 1, banks[1], False)
+        gradient(1, 1, 1, banks[2], False)
+        gradient(0, 1, 1, banks[3], False)
+        head_block(1)
+        tail_piece(0, 3)
+        tail_piece(1, 2)
+        gradient(0, 0, 2, banks[4], False)
+        gradient(1, 0, 2, banks[5], False)
+        gradient(1, 1, 2, banks[6], True)
+        head_block(2)
+        tail_piece(2, 0)
+        tail_piece(1, 3)
+        gradient(0, 1, 2, banks[7], False)
+        gradient(0, 0, 3, banks[0], False)
+        tail_piece(2, 1)
+        tail_piece(3, 0)
+        tail_piece(2, 2)
+        gradient(0, 1, 3, banks[1], False)
+        gradient(1, 0, 3, banks[2], True)
+        gradient(1, 1, 3, banks[3], True)
+        tail_piece(3, 1)
+        tail_piece(2, 3)
+        tail_piece(3, 2)
+        tail_piece(3, 3)
+        head_block(3)

@@ -117,14 +117,12 @@ def tile_attend_gmf_nce_vu_kernel(tc, uT, vT, y, us, ts, offs, uoffs, out_0, out
                     nc.sync.dma_start(row_scale[:], us.rearrange("b (p t) o -> p b (t o)", t=PACK))
 
         nc.vector.memset(tail_scale_row[0 : P - 1, :], 0.0)
-        windows = [held("window%d" % j, [P, T]) for j in range(5)]
-        for window in windows[0:2]:
+        windows = [held("window%d" % j, [P, T]) for j in range(3)]
+        for window in windows:
             nc.vector.memset(window[:], 0.0)
-        for window in windows[2:]:
-            nc.gpsimd.memset(window[:], 0.0)
 
         picked = placed("picked", [P, LISTED], 80)
-        gather(True, picked[:], tail_scale_row, tail_list, 0, LISTED)
+        gather(False, picked[:], tail_scale_row, tail_list, 0, LISTED)
         labels = []
         for b in range(B):
             labels.append(placed("labels%d" % b, [P, PACK, N], 64 + 8 * b))
@@ -132,8 +130,10 @@ def tile_attend_gmf_nce_vu_kernel(tc, uT, vT, y, us, ts, offs, uoffs, out_0, out
         for b in range(B):
             transposes(banks[b], lambda j: picked[:, b * N + j * P : b * N + (j + 1) * P])
             nc.vector.tensor_copy(slot_scale[:, b, :], banks[b][:, :, P - 1])
+        windows.append(placed("window3", [P, T], 80))
+        nc.gpsimd.memset(windows[3][:], 0.0)
         nc.gpsimd.tensor_scalar(half_scale[:], row_scale[:], 0.5, 0.0, MULT, ADD)
-        slot_row = placed("slot_row", [P, LISTED], 84)
+        slot_row = placed("slot_row", [P, LISTED], 176)
         half_sc = []
         for b in range(B):
             transposes(banks[2 + b], lambda j: slot_scale[:, b, j : j + 1].to_broadcast([P, P]))
@@ -149,11 +149,11 @@ def tile_attend_gmf_nce_vu_kernel(tc, uT, vT, y, us, ts, offs, uoffs, out_0, out
         xq = [operand("xq%d" % b, K) for b in range(B)]
         wq = [operand("wq%d" % b, K) for b in range(B)]
         xr = [operand("xr%d" % t, B * P) for t in range(PACK)]
-        wi = [operand("wi%d" % t, B * P) for t in range(2)]
-        wi_late = operand("wi_late", 2 * B * P)
-        for t in range(2):
-            cols = slice(t * B * P, (t + 1) * B * P)
-            wi.append((wi_late[0][:, cols], wi_late[1][:, cols]))
+        wi_pairs = [operand("wi%d" % j, 2 * B * P) for j in range(2)]
+        wi = []
+        for t in range(PACK):
+            cols = slice(t % 2 * B * P, (t % 2 + 1) * B * P)
+            wi.append((wi_pairs[t // 2][0][:, cols], wi_pairs[t // 2][1][:, cols]))
 
         def plane(planes, t):
             return planes[:, t * LISTED : (t + 1) * LISTED]
@@ -177,24 +177,18 @@ def tile_attend_gmf_nce_vu_kernel(tc, uT, vT, y, us, ts, offs, uoffs, out_0, out
         for b in range(B):
             quantize(xq[b], x[b][:], E4M3)
 
-        w_turned = [placed("w_turned%d" % t, [P, K], 128 + 2 * t) for t in range(2)]
         for t in range(PACK - 1):
             gather(False, plane(w_planes, t), tables[1][t], tail_list, 0, LISTED)
-            if t < 2:
-                turn_plane(True, w_turned[t][:], plane(w_planes, t), banks[4 + t])
-                quantize(wi[t], w_turned[t][:].bitcast(BF16), E4M3)
         last = PACK - 1
-        for b in range(B):
-            gather(b == 0, plane(w_planes, last)[:, b * N : (b + 1) * N], tables[1][last], tail_list, b * N, N)
+        for on_vector, first, count in ((True, 0, PIECE), (False, PIECE, PIECE), (False, N, N)):
+            gather(on_vector, plane(w_planes, last)[:, first : first + count], tables[1][last], tail_list, first, count)
         w = [placed("w%d" % b, [P, K * PACK], 144 + 4 * b, BF16) for b in range(B)]
         interleave(w[0], group_planes(w_planes, 0))
         quantize(wq[0], w[0][:], E4M3)
-        w_late = placed("w_late", [P, 2 * K], 56)
-        for t in range(2):
-            turn_plane(False, w_late[:, t * K : (t + 1) * K], plane(w_planes, 2 + t), banks[6 + t])
+        w_turned = [placed("w_turned%d" % j, [P, 2 * K], 56 + 4 * j) for j in range(2)]
+        for t in range(PACK):
+            turn_plane(False, w_turned[t // 2][:, t % 2 * K : (t % 2 + 1) * K], plane(w_planes, t), banks[4 + t])
         interleave(w[1], group_planes(w_planes, 1))
-        quantize(wi_late, w_late[:].bitcast(BF16), E4M3)
-        quantize(wq[1], w[1][:], E4M3)
 
         logits = placed("logits", [P, PACK, R], 152)
         prob = [placed("prob%d" % b, [P, PACK, N], 160 + 8 * b) for b in range(B)]
@@ -207,21 +201,22 @@ def tile_attend_gmf_nce_vu_kernel(tc, uT, vT, y, us, ts, offs, uoffs, out_0, out
         def scores(b, first_banks, second_banks):
             for j, bank in enumerate(first_banks):
                 product(bank, wq[b], block(j), xq[b], E4M3)
-                nc.scalar.activation(logits[:, j, :], flat(bank), COPY, scale=slot_scale[:, b, j : j + 1])
+                scale = slot_scale[:, b, j : j + 1]
+                if b == 0 and j % 2 == 1:
+                    nc.vector.tensor_scalar(logits[:, j, :], flat(bank), scale, None, MULT)
+                else:
+                    nc.scalar.activation(logits[:, j, :], flat(bank), COPY, scale=scale)
             for t, bank in enumerate(second_banks):
                 transposes(bank, lambda j: logits[:, j, block(t)])
                 nc.scalar.activation(prob[b][:, t, :], flat(bank), TANH, scale=half_scale[:, b, t : t + 1])
 
         def weights(b):
             planes = h_planes[b][:].rearrange("p (t i) -> p t i", t=PACK)
-            for t in range(PACK + 1):
-                if t < PACK:
-                    part = prob[b][:, t, :]
-                    nc.vector.scalar_tensor_tensor(part, labels[b][:, t, :], -2.0, part, MULT, ADD)
-                if t > 0:
-                    nc.vector.scalar_tensor_tensor(
-                        planes[:, t - 1, :], prob[b][:, t - 1, :], 1.0, half_sc[b][:, t - 1, :], ADD, MULT
-                    )
+            for ts_ in (slice(0, 1), slice(1, 2), slice(2, 4)):
+                part = prob[b][:, ts_, :]
+                nc.vector.scalar_tensor_tensor(part, labels[b][:, ts_, :], -2.0, part, MULT, ADD)
+            for ts_ in (slice(0, 2), slice(2, 4)):
+                nc.vector.scalar_tensor_tensor(planes[:, ts_, :], prob[b][:, ts_, :], 1.0, half_sc[b][:, ts_, :], ADD, MULT)
             interleave(h[b], planes)
             quantize(hr[b], h[b][:], E5M2)
 
@@ -240,61 +235,66 @@ def tile_attend_gmf_nce_vu_kernel(tc, uT, vT, y, us, ts, offs, uoffs, out_0, out
         def store(out, t, window):
             nc.sync.dma_start(out.rearrange("(p t) c -> p t c", t=PACK)[:, t, :], window[:])
 
-        def tail_piece(t, c):
-            window = windows[t % 3]
-            first = c * PIECE
+        def tail_piece(t, first, count):
+            window = tail_windows[t]
             nc.scalar.activation(
-                window[:].indirect(entries(tail_list, first, PIECE)), stages[0][t][:, first : first + PIECE], COPY
+                window[:].indirect(entries(tail_list, first, count)), stages[0][t][:, first : first + count], COPY
             )
-            if c == PACK - 1:
+            if first + count == LISTED:
                 store(out_0, t, window)
 
         def head_block(t):
-            window = windows[3 + t % 2]
+            window = head_windows[t % 2]
             nc.vector.tensor_copy(window[:].indirect(head_list[:]), stages[1][t][:])
             store(out_1, t, window)
 
         scores(0, banks[0:4], banks[4:8])
+        quantize(wq[1], w[1][:], E4M3)
+        for j in range(2):
+            quantize(wi_pairs[j], w_turned[j][:].bitcast(BF16), E4M3)
         weights(0)
         scores(1, banks[4:8], banks[0:4])
+        tail_windows = [windows[0], windows[1], windows[3]]
+        head_windows = [windows[2]]
         turn_weights(0, banks[4:6])
         gradient(0, 0, 0, banks[6], False)
-        tail_piece(0, 0)
-        tail_piece(0, 1)
+        tail_piece(0, 0, 256)
+        tail_piece(0, 256, 256)
         weights(1)
         quantize(hi[0], h_turned[0][:].bitcast(BF16), E5M2)
         turn_weights(1, banks[4:6])
         gradient(1, 0, 0, banks[7], True)
         quantize(hi[1], h_turned[1][:].bitcast(BF16), E5M2)
+        for side, name, kib in ((head_windows, "window4", 126), (tail_windows, "window5", 118)):
+            side.append(placed(name, [P, T], kib))
+            nc.gpsimd.memset(side[-1][:], 0.0)
         gradient(0, 0, 1, banks[4], False)
-        tail_piece(1, 0)
+        tail_piece(1, 0, 256)
         gradient(1, 1, 0, banks[0], True)
         head_block(0)
         gradient(0, 1, 0, banks[5], False)
-        tail_piece(1, 1)
-        tail_piece(0, 2)
+        tail_piece(1, 256, 256)
+        tail_piece(0, 512, 256)
         gradient(1, 0, 1, banks[1], False)
         gradient(1, 1, 1, banks[2], False)
         gradient(0, 1, 1, banks[3], False)
         head_block(1)
-        tail_piece(0, 3)
-        tail_piece(1, 2)
+        tail_piece(0, 768, 256)
+        tail_piece(1, 512, 256)
         gradient(0, 0, 2, banks[4], False)
-        gradient(1, 0, 2, banks[5], False)
-        gradient(1, 1, 2, banks[6], True)
+        gradient(0, 1, 2, banks[5], False)
+        gradient(1, 0, 2, banks[6], False)
+        gradient(1, 1, 2, banks[7], True)
         head_block(2)
-        tail_piece(2, 0)
-        tail_piece(1, 3)
-        gradient(0, 1, 2, banks[7], False)
+        tail_piece(2, 0, 384)
+        tail_piece(1, 768, 256)
         gradient(0, 0, 3, banks[0], False)
-        tail_piece(2, 1)
-        tail_piece(3, 0)
-        tail_piece(2, 2)
         gradient(0, 1, 3, banks[1], False)
+        tail_piece(2, 384, 384)
+        tail_piece(3, 0, 384)
+        tail_piece(2, 768, 256)
         gradient(1, 0, 3, banks[2], True)
         gradient(1, 1, 3, banks[3], True)
-        tail_piece(3, 1)
-        tail_piece(2, 3)
-        tail_piece(3, 2)
-        tail_piece(3, 3)
+        tail_piece(3, 384, 384)
+        tail_piece(3, 768, 256)
         head_block(3)

@@ -97,9 +97,11 @@ def tile_attend_gmf_nce_vu_kernel(tc, uT, vT, y, us, ts, offs, uoffs, out_0, out
             transposes(bank, lambda a: words[:, a // 2, a % 2, :])
             copy(on_vector, dst.rearrange("q (b p u) -> q b p u", b=B, u=2), bank[:].rearrange("q (b u) p -> q b p u", u=2))
 
-        def interleave(dst, planes):
-            nc.vector.tensor_copy(
-                dst[:].rearrange("p (q s t) -> p q t s", s=PACK, t=PACK), planes.rearrange("p t (q s) -> p q t s", s=PACK)
+        def interleave(on_vector, dst, planes):
+            copy(
+                on_vector,
+                dst[:].rearrange("p (q s t) -> p q t s", s=PACK, t=PACK),
+                planes.rearrange("p t (q s) -> p q t s", s=PACK),
             )
 
         tail_scale_row = placed("tail_scale_row", [P, T], 64)
@@ -114,8 +116,11 @@ def tile_attend_gmf_nce_vu_kernel(tc, uT, vT, y, us, ts, offs, uoffs, out_0, out
                 nc.sync.dma_start(tables[side][t][:], rows[:, t, :])
                 if side == 0 and t == 0:
                     nc.sync.dma_start(head_list[:], uoffs)
-                    nc.sync.dma_start(row_scale[:], us.rearrange("b (p t) o -> p b (t o)", t=PACK))
 
+        warm = held("warm", [P, 2])
+        nc.gpsimd.memset(warm[:, 0:1], 0.0)
+        nc.scalar.activation(warm[:, 1:2], warm[:, 0:1], TANH)
+        nc.scalar.dma_start(row_scale[:], us.rearrange("b (p t) o -> p b (t o)", t=PACK))
         nc.vector.memset(tail_scale_row[0 : P - 1, :], 0.0)
         windows = [held("window%d" % j, [P, T]) for j in range(3)]
         for window in windows:
@@ -147,13 +152,10 @@ def tile_attend_gmf_nce_vu_kernel(tc, uT, vT, y, us, ts, offs, uoffs, out_0, out
         x_planes = placed("x_planes", [P, PACK * LISTED], 104, BF16)
         w_planes = placed("w_planes", [P, PACK * LISTED], 112, BF16)
         xq = [operand("xq%d" % b, K) for b in range(B)]
-        wq = [operand("wq%d" % b, K) for b in range(B)]
-        xr = [operand("xr%d" % t, B * P) for t in range(PACK)]
-        wi_pairs = [operand("wi%d" % j, 2 * B * P) for j in range(2)]
-        wi = []
-        for t in range(PACK):
-            cols = slice(t % 2 * B * P, (t % 2 + 1) * B * P)
-            wi.append((wi_pairs[t // 2][0][:, cols], wi_pairs[t // 2][1][:, cols]))
+        wq_both = operand("wq", B * K)
+        wq = [(wq_both[0][:, b * K : (b + 1) * K], wq_both[1][:, b * K : (b + 1) * K]) for b in range(B)]
+        xr = operand("xr", B * K)
+        wi = operand("wi", B * K)
 
         def plane(planes, t):
             return planes[:, t * LISTED : (t + 1) * LISTED]
@@ -161,21 +163,20 @@ def tile_attend_gmf_nce_vu_kernel(tc, uT, vT, y, us, ts, offs, uoffs, out_0, out
         def group_planes(planes, b):
             return planes[:].rearrange("p (t b i) -> p b t i", t=PACK, b=B)[:, b]
 
-        x_turned = []
+        x_turned = placed("x_turned", [P, PACK * K], 120)
         for t in range(PACK):
-            gather(t == 2, plane(x_planes, t), tables[0][t], head_list, 0, LISTED)
-            x_turned.append(placed("x_turned%d" % t, [P, K], 120 + 2 * t))
-            turn_plane(True, x_turned[t][:], plane(x_planes, t), banks[4 + t])
+            if t < PACK - 1:
+                gather(t == 2, plane(x_planes, t), tables[0][t], head_list, 0, LISTED)
+            else:
+                for b in range(B):
+                    gather(b == 0, plane(x_planes, t)[:, b * K : (b + 1) * K], tables[0][t], head_list, b * K, K)
+            turn_plane(True, x_turned[:, t * K : (t + 1) * K], plane(x_planes, t), banks[4 + t])
         x = [placed("x%d" % b, [P, K * PACK], 136 + 4 * b, BF16) for b in range(B)]
         for b in range(B):
-            nc.vector.tensor_copy(
-                x[b][:].rearrange("p (s q t) -> p q s t", s=PACK, t=PACK),
-                group_planes(x_planes, b).rearrange("p t (q s) -> p q s t", s=PACK),
-            )
-        for t in range(PACK):
-            quantize(xr[t], x_turned[t][:].bitcast(BF16), E4M3)
+            interleave(True, x[b], group_planes(x_planes, b))
         for b in range(B):
             quantize(xq[b], x[b][:], E4M3)
+        quantize(xr, x_turned[:].bitcast(BF16), E4M3)
 
         for t in range(PACK - 1):
             gather(False, plane(w_planes, t), tables[1][t], tail_list, 0, LISTED)
@@ -183,29 +184,33 @@ def tile_attend_gmf_nce_vu_kernel(tc, uT, vT, y, us, ts, offs, uoffs, out_0, out
         for on_vector, first, count in ((True, 0, PIECE), (False, PIECE, PIECE), (False, N, N)):
             gather(on_vector, plane(w_planes, last)[:, first : first + count], tables[1][last], tail_list, first, count)
         w = [placed("w%d" % b, [P, K * PACK], 144 + 4 * b, BF16) for b in range(B)]
-        interleave(w[0], group_planes(w_planes, 0))
+        interleave(True, w[0], group_planes(w_planes, 0))
         quantize(wq[0], w[0][:], E4M3)
-        w_turned = [placed("w_turned%d" % j, [P, 2 * K], 56 + 4 * j) for j in range(2)]
+        interleave(False, w[1], group_planes(w_planes, 1))
+        w_turned = placed("w_turned", [P, PACK * K], 56)
         for t in range(PACK):
-            turn_plane(False, w_turned[t // 2][:, t % 2 * K : (t % 2 + 1) * K], plane(w_planes, t), banks[4 + t])
-        interleave(w[1], group_planes(w_planes, 1))
+            turn_plane(True, w_turned[:, t * K : (t + 1) * K], plane(w_planes, t), banks[4 + t])
 
         logits = placed("logits", [P, PACK, R], 152)
         prob = [placed("prob%d" % b, [P, PACK, N], 160 + 8 * b) for b in range(B)]
         h_planes = [placed("h_planes%d" % b, [P, PACK * N], 104 + 4 * b, BF16) for b in range(B)]
         h = [placed("h%d" % b, [P, K * PACK], 136 + 4 * b, BF16) for b in range(B)]
-        h_turned = [placed("h_turned%d" % b, [P, 2 * K], 120 + 4 * b) for b in range(B)]
+        h_turned = placed("h_turned", [P, B * 2 * K], 120)
         hr, hi = xq, wq
-        stages = [[placed("stage%d_%d" % (o, t), [P, LISTED], 32 + 16 * o + 4 * t) for t in range(PACK)] for o in range(2)]
+        stages = [[placed("stage%d_%d" % (o, t), [P, LISTED], (8 + 8 * t, 40 + 4 * t)[o]) for t in range(PACK)] for o in range(2)]
 
-        def scores(b, first_banks, second_banks):
+        def scores(b, first_banks):
             for j, bank in enumerate(first_banks):
                 product(bank, wq[b], block(j), xq[b], E4M3)
                 scale = slot_scale[:, b, j : j + 1]
+                dst = logits[:, j, :].rearrange("p (t q) -> p t q", t=PACK)
+                src = flat(bank).rearrange("p (q t) -> p t q", t=PACK)
                 if b == 0 and j % 2 == 1:
-                    nc.vector.tensor_scalar(logits[:, j, :], flat(bank), scale, None, MULT)
+                    nc.vector.tensor_scalar(dst, src, scale, None, MULT)
                 else:
-                    nc.scalar.activation(logits[:, j, :], flat(bank), COPY, scale=scale)
+                    nc.scalar.activation(dst, src, COPY, scale=scale)
+
+        def squash(b, second_banks):
             for t, bank in enumerate(second_banks):
                 transposes(bank, lambda j: logits[:, j, block(t)])
                 nc.scalar.activation(prob[b][:, t, :], flat(bank), TANH, scale=half_scale[:, b, t : t + 1])
@@ -217,84 +222,83 @@ def tile_attend_gmf_nce_vu_kernel(tc, uT, vT, y, us, ts, offs, uoffs, out_0, out
                 nc.vector.scalar_tensor_tensor(part, labels[b][:, ts_, :], -2.0, part, MULT, ADD)
             for ts_ in (slice(0, 2), slice(2, 4)):
                 nc.vector.scalar_tensor_tensor(planes[:, ts_, :], prob[b][:, ts_, :], 1.0, half_sc[b][:, ts_, :], ADD, MULT)
-            interleave(h[b], planes)
+            interleave(True, h[b], planes)
             quantize(hr[b], h[b][:], E5M2)
 
-        def turn_weights(b, two_banks):
+        def turn_weights(on_vector, b, two_banks):
             words = h_planes[b][:].bitcast(F32).rearrange("p (t q u) -> p t u q", t=PACK, u=2)
             for j, bank in enumerate(two_banks):
                 transposes(bank, lambda a: words[:, 2 * j + a // 2, a % 2, :])
-                nc.scalar.copy(
-                    h_turned[b][:].rearrange("q (p j a) -> q j p a", j=2, a=PACK)[:, j], bank[:].rearrange("q a p -> q p a")
-                )
+                dst = h_turned[:].rearrange("q (b p j a) -> q b j p a", b=B, j=2, a=PACK)[:, b, j]
+                copy(on_vector, dst, bank[:].rearrange("q a p -> q p a"))
 
         def gradient(o, b, t, bank, on_vector):
-            product(bank, (xr, wi)[o][t], block(b), (hr, hi)[o][b], E5M2)
+            product(bank, (xr, wi)[o], block(B * t + b), (hr, hi)[o][b], E5M2)
             copy(on_vector, stages[o][t][:, b * K : (b + 1) * K], flat(bank))
 
-        def store(out, t, window):
-            nc.sync.dma_start(out.rearrange("(p t) c -> p t c", t=PACK)[:, t, :], window[:])
+        late_windows = [None] * PACK
 
-        def tail_piece(t, first, count):
-            window = tail_windows[t]
-            nc.scalar.activation(
-                window[:].indirect(entries(tail_list, first, count)), stages[0][t][:, first : first + count], COPY
-            )
+        def scatter(on_vector, o, t, first, count):
+            out, lst = ((out_0, tail_list), (out_1, head_list))[o]
+            window = (windows, late_windows)[o][t]
+            dst, src = window[:].indirect(entries(lst, first, count)), stages[o][t][:, first : first + count]
+            if on_vector:
+                nc.vector.tensor_copy(dst, src)
+            else:
+                nc.scalar.activation(dst, src, COPY)
             if first + count == LISTED:
-                store(out_0, t, window)
+                nc.sync.dma_start(out.rearrange("(p t) c -> p t c", t=PACK)[:, t, :], window[:])
 
-        def head_block(t):
-            window = head_windows[t % 2]
-            nc.vector.tensor_copy(window[:].indirect(head_list[:]), stages[1][t][:])
-            store(out_1, t, window)
+        def zeroed_window(t, kib):
+            late_windows[t] = placed("late_window%d" % t, [P, T], kib)
+            nc.gpsimd.memset(late_windows[t][:], 0.0)
 
-        scores(0, banks[0:4], banks[4:8])
+        scores(0, banks[0:4])
+        squash(0, banks[4:8])
         quantize(wq[1], w[1][:], E4M3)
-        for j in range(2):
-            quantize(wi_pairs[j], w_turned[j][:].bitcast(BF16), E4M3)
         weights(0)
-        scores(1, banks[4:8], banks[0:4])
-        tail_windows = [windows[0], windows[1], windows[3]]
-        head_windows = [windows[2]]
-        turn_weights(0, banks[4:6])
-        gradient(0, 0, 0, banks[6], False)
-        tail_piece(0, 0, 256)
-        tail_piece(0, 256, 256)
+        scores(1, banks[4:8])
+        squash(1, banks[0:4])
+        turn_weights(False, 0, banks[4:6])
+        gradient(0, 0, 2, banks[6], False)
+        scatter(False, 0, 2, 0, 256)
+        gradient(0, 0, 3, banks[7], False)
+        scatter(False, 0, 3, 0, 256)
+        scatter(False, 0, 2, 256, 256)
         weights(1)
-        quantize(hi[0], h_turned[0][:].bitcast(BF16), E5M2)
-        turn_weights(1, banks[4:6])
-        gradient(1, 0, 0, banks[7], True)
-        quantize(hi[1], h_turned[1][:].bitcast(BF16), E5M2)
-        for side, name, kib in ((head_windows, "window4", 126), (tail_windows, "window5", 118)):
-            side.append(placed(name, [P, T], kib))
-            nc.gpsimd.memset(side[-1][:], 0.0)
-        gradient(0, 0, 1, banks[4], False)
-        tail_piece(1, 0, 256)
-        gradient(1, 1, 0, banks[0], True)
-        head_block(0)
-        gradient(0, 1, 0, banks[5], False)
-        tail_piece(1, 256, 256)
-        tail_piece(0, 512, 256)
-        gradient(1, 0, 1, banks[1], False)
-        gradient(1, 1, 1, banks[2], False)
-        gradient(0, 1, 1, banks[3], False)
-        head_block(1)
-        tail_piece(0, 768, 256)
-        tail_piece(1, 512, 256)
-        gradient(0, 0, 2, banks[4], False)
-        gradient(0, 1, 2, banks[5], False)
-        gradient(1, 0, 2, banks[6], False)
-        gradient(1, 1, 2, banks[7], True)
-        head_block(2)
-        tail_piece(2, 0, 384)
-        tail_piece(1, 768, 256)
-        gradient(0, 0, 3, banks[0], False)
-        gradient(0, 1, 3, banks[1], False)
-        tail_piece(2, 384, 384)
-        tail_piece(3, 0, 384)
-        tail_piece(2, 768, 256)
-        gradient(1, 0, 3, banks[2], True)
-        gradient(1, 1, 3, banks[3], True)
-        tail_piece(3, 384, 384)
-        tail_piece(3, 768, 256)
-        head_block(3)
+        quantize(wi, w_turned[:].bitcast(BF16), E4M3)
+        turn_weights(True, 1, banks[4:6])
+        quantize(wq_both, h_turned[:].bitcast(BF16), E5M2)
+        zeroed_window(0, 113)
+        zeroed_window(2, 121)
+        gradient(0, 1, 0, banks[2], True)
+        gradient(0, 0, 0, banks[1], False)
+        gradient(0, 1, 2, banks[0], False)
+        scatter(True, 0, 0, 0, LISTED)
+        zeroed_window(1, 2)
+        scatter(False, 0, 2, 512, 256)
+        scatter(False, 0, 3, 256, 256)
+        scatter(False, 0, 2, 768, 256)
+        zeroed_window(3, 24)
+        gradient(0, 0, 1, banks[3], False)
+        gradient(0, 1, 1, banks[6], False)
+        gradient(0, 1, 3, banks[7], False)
+        scatter(True, 0, 1, 0, LISTED)
+        scatter(False, 0, 3, 512, 256)
+        gradient(1, 0, 0, banks[4], False)
+        scatter(False, 0, 3, 768, 256)
+        gradient(1, 1, 0, banks[5], True)
+        gradient(1, 0, 2, banks[0], False)
+        gradient(1, 1, 2, banks[1], False)
+        scatter(True, 1, 0, 0, LISTED)
+        scatter(False, 1, 2, 0, 384)
+        gradient(1, 0, 3, banks[2], False)
+        scatter(False, 1, 2, 384, 384)
+        gradient(1, 1, 3, banks[3], False)
+        scatter(False, 1, 2, 768, 256)
+        gradient(1, 0, 1, banks[6], True)
+        gradient(1, 1, 1, banks[7], True)
+        scatter(False, 1, 3, 0, 384)
+        scatter(False, 1, 3, 384, 384)
+        scatter(False, 1, 3, 768, 256)
+        scatter(True, 1, 1, 0, LISTED)

from contextlib import ExitStack

import concourse.mybir as mybir
from concourse.masks import make_identity

B, N, T, D, R, TU = 2, 512, 2048, 512, 512, 2048
FLOPS = 3 * 2 * B * R * N * D

F32 = mybir.dt.float32
BF16 = mybir.dt.bfloat16
U32 = mybir.dt.uint32
U16 = mybir.dt.uint16
U8 = mybir.dt.uint8
E4M3 = mybir.dt.float8_e4m3fn_x4
E5M2 = mybir.dt.float8_e5m2_x4
MULT = mybir.AluOpType.mult
ADD = mybir.AluOpType.add
COPY = mybir.ActivationFunctionType.Copy
TANH = mybir.ActivationFunctionType.Tanh

P = 128
PACK = 4
K = P * PACK
LISTED = B * K
PIECE = 256
KIB = 1024


def tile_attend_gmf_nce_vu_kernel(tc, uT, vT, y, us, ts, offs, uoffs, out_0, out_1):
    nc = tc.nc
    with ExitStack() as ctx:
        keep = ctx.enter_context(tc.tile_pool(name="keep", bufs=1))
        shared = ctx.enter_context(tc.tile_pool(name="shared", bufs=1))
        psum = ctx.enter_context(tc.psum_pool(name="psum", bufs=1))

        banks = [psum.tile([P, PACK, P], F32, name="bank%d" % j) for j in range(8)]

        def held(name, shape, dtype=F32):
            return keep.tile(shape, dtype, name=name, align_bytes=64)

        def placed(name, shape, kib, dtype=F32):
            return shared.tile(shape, dtype, name=name, align_bytes=64, offset=int(kib * KIB))

        def operand(name, columns):
            return held(name + "_codes", [P, columns], U32), held(name + "_scales", [P, columns], U8)

        def flat(bank):
            return bank[:].rearrange("p s q -> p (s q)")

        head_list = keep.tile([P, LISTED // 16], U16, name="head_list")
        tail_list = keep.tile([P, LISTED // 16], U16, name="tail_list")
        row_scale = held("row_scale", [P, B, PACK])
        half_scale = held("half_scale", [P, B, PACK])
        slot_scale = held("slot_scale", [P, B, PACK])
        ident = held("ident", [P, P])
        make_identity(nc, ident[:])

        def entries(lst, first, count):
            return lst[:, first // 16 : (first + count) // 16]

        def gather(on_vector, dst, table, lst, first, count):
            src = table[:].indirect(entries(lst, first, count))
            if on_vector:
                nc.vector.tensor_copy(dst, src)
            else:
                nc.scalar.activation(dst, src, COPY)

        def quantize(op, src, fmt):
            nc.vector.quantize_mx(op[0][:].bitcast(fmt), op[1][:], src)

        def product(bank, stationary, cols, moving, moving_fmt):
            nc.tensor.matmul_mx(
                flat(bank),
                lhsT=stationary[0][:, cols].bitcast(E4M3),
                lhsT_scale=stationary[1][:, cols],
                rhs=moving[0][:].bitcast(moving_fmt),
                rhs_scale=moving[1][:],
                start=True,
                stop=True,
            )

        def transposes(bank, source):
            for s in range(PACK):
                nc.tensor.transpose(bank[:, s, :], source(s), ident[:])

        def block(j):
            return slice(j * P, (j + 1) * P)

        def copy(on_vector, dst, src):
            if on_vector:
                nc.vector.tensor_copy(dst, src)
            else:
                nc.scalar.copy(dst, src)

        def turn_plane(on_vector, dst, plane, bank):
            words = plane.bitcast(F32).rearrange("p (b q u) -> p b u q", b=B, u=2)
            transposes(bank, lambda a: words[:, a // 2, a % 2, :])
            copy(on_vector, dst.rearrange("q (b p u) -> q b p u", b=B, u=2), bank[:].rearrange("q (b u) p -> q b p u", u=2))

        def interleave(on_vector, dst, planes):
            copy(
                on_vector,
                dst[:].rearrange("p (q s t) -> p q t s", s=PACK, t=PACK),
                planes.rearrange("p t (q s) -> p q t s", s=PACK),
            )

        tail_scale_row = placed("tail_scale_row", [P, T], 64)
        nc.sync.dma_start(tail_scale_row[P - 1 : P, :], ts[0:1, :])
        nc.sync.dma_start(tail_list[:], offs)
        tables = []
        for side, table in enumerate((uT, vT)):
            rows = table.rearrange("(p t) c -> p t c", t=PACK)
            tables.append([])
            for t in range(PACK):
                tables[side].append(placed("table%d_%d" % (side, t), [P, T], 32 * side + 8 * t))
                nc.sync.dma_start(tables[side][t][:], rows[:, t, :])
                if side == 0 and t == 0:
                    nc.sync.dma_start(head_list[:], uoffs)

        warm = held("warm", [P, 2])
        nc.gpsimd.memset(warm[:, 0:1], 0.0)
        nc.scalar.activation(warm[:, 1:2], warm[:, 0:1], TANH)
        nc.scalar.dma_start(row_scale[:], us.rearrange("b (p t) o -> p b (t o)", t=PACK))
        nc.vector.memset(tail_scale_row[0 : P - 1, :], 0.0)
        windows = [held("window%d" % j, [P, T]) for j in range(3)]
        for window in windows:
            nc.vector.memset(window[:], 0.0)

        picked = placed("picked", [P, LISTED], 80)
        gather(False, picked[:], tail_scale_row, tail_list, 0, LISTED)
        labels = []
        for b in range(B):
            labels.append(placed("labels%d" % b, [P, PACK, N], 64 + 8 * b))
            nc.sync.dma_start(labels[b][:], y[b].rearrange("(p t) i -> p t i", t=PACK))
        for b in range(B):
            transposes(banks[b], lambda j: picked[:, b * N + j * P : b * N + (j + 1) * P])
            nc.vector.tensor_copy(slot_scale[:, b, :], banks[b][:, :, P - 1])
        windows.append(placed("window3", [P, T], 80))
        nc.gpsimd.memset(windows[3][:], 0.0)
        nc.gpsimd.tensor_scalar(half_scale[:], row_scale[:], 0.5, 0.0, MULT, ADD)
        slot_row = placed("slot_row", [P, LISTED], 176)
        half_sc = []
        for b in range(B):
            transposes(banks[2 + b], lambda j: slot_scale[:, b, j : j + 1].to_broadcast([P, P]))
            nc.vector.tensor_copy(slot_row[:, b * N : (b + 1) * N], flat(banks[2 + b]))
            half_sc.append(placed("half_sc%d" % b, [P, PACK, N], 88 + 8 * b))
            for t in range(PACK):
                nc.gpsimd.tensor_scalar(
                    half_sc[b][:, t, :], slot_row[:, b * N : (b + 1) * N], half_scale[:, b, t : t + 1], 0.0, MULT, ADD
                )

        x_planes = placed("x_planes", [P, PACK * LISTED], 104, BF16)
        w_planes = placed("w_planes", [P, PACK * LISTED], 112, BF16)
        xq = [operand("xq%d" % b, K) for b in range(B)]
        wq_both = operand("wq", B * K)
        wq = [(wq_both[0][:, b * K : (b + 1) * K], wq_both[1][:, b * K : (b + 1) * K]) for b in range(B)]
        xr = operand("xr", B * K)
        wi = operand("wi", B * K)

        def plane(planes, t):
            return planes[:, t * LISTED : (t + 1) * LISTED]

        def group_planes(planes, b):
            return planes[:].rearrange("p (t b i) -> p b t i", t=PACK, b=B)[:, b]

        x_turned = placed("x_turned", [P, PACK * K], 120)
        for t in range(PACK):
            if t < PACK - 1:
                gather(t == 2, plane(x_planes, t), tables[0][t], head_list, 0, LISTED)
            else:
                for b in range(B):
                    gather(b == 0, plane(x_planes, t)[:, b * K : (b + 1) * K], tables[0][t], head_list, b * K, K)
            turn_plane(True, x_turned[:, t * K : (t + 1) * K], plane(x_planes, t), banks[4 + t])
        x = [placed("x%d" % b, [P, K * PACK], 136 + 4 * b, BF16) for b in range(B)]
        for b in range(B):
            interleave(True, x[b], group_planes(x_planes, b))
        for b in range(B):
            quantize(xq[b], x[b][:], E4M3)
        quantize(xr, x_turned[:].bitcast(BF16), E4M3)

        for t in range(PACK - 1):
            gather(False, plane(w_planes, t), tables[1][t], tail_list, 0, LISTED)
        last = PACK - 1
        for on_vector, first, count in ((True, 0, PIECE), (False, PIECE, PIECE), (False, N, N)):
            gather(on_vector, plane(w_planes, last)[:, first : first + count], tables[1][last], tail_list, first, count)
        w = [placed("w%d" % b, [P, K * PACK], 144 + 4 * b, BF16) for b in range(B)]
        interleave(True, w[0], group_planes(w_planes, 0))
        quantize(wq[0], w[0][:], E4M3)
        interleave(False, w[1], group_planes(w_planes, 1))
        w_turned = placed("w_turned", [P, PACK * K], 56)
        for t in range(PACK):
            turn_plane(True, w_turned[:, t * K : (t + 1) * K], plane(w_planes, t), banks[4 + t])

        logits = placed("logits", [P, PACK, R], 152)
        prob = [placed("prob%d" % b, [P, PACK, N], 160 + 8 * b) for b in range(B)]
        h_planes = [placed("h_planes%d" % b, [P, PACK * N], 104 + 4 * b, BF16) for b in range(B)]
        h = [placed("h%d" % b, [P, K * PACK], 136 + 4 * b, BF16) for b in range(B)]
        h_turned = placed("h_turned", [P, B * 2 * K], 120)
        hr, hi = xq, wq
        stages = [[placed("stage%d_%d" % (o, t), [P, LISTED], (8 + 8 * t, 40 + 4 * t)[o]) for t in range(PACK)] for o in range(2)]

        def scores(b, first_banks):
            for j, bank in enumerate(first_banks):
                product(bank, wq[b], block(j), xq[b], E4M3)
                scale = slot_scale[:, b, j : j + 1]
                dst = logits[:, j, :].rearrange("p (t q) -> p t q", t=PACK)
                src = flat(bank).rearrange("p (q t) -> p t q", t=PACK)
                if b == 0 and j % 2 == 1:
                    nc.vector.tensor_scalar(dst, src, scale, None, MULT)
                else:
                    nc.scalar.activation(dst, src, COPY, scale=scale)

        def squash(b, second_banks):
            for t, bank in enumerate(second_banks):
                transposes(bank, lambda j: logits[:, j, block(t)])
                nc.scalar.activation(prob[b][:, t, :], flat(bank), TANH, scale=half_scale[:, b, t : t + 1])

        def weights(b):
            planes = h_planes[b][:].rearrange("p (t i) -> p t i", t=PACK)
            for ts_ in (slice(0, 1), slice(1, 2), slice(2, 4)):
                part = prob[b][:, ts_, :]
                nc.vector.scalar_tensor_tensor(part, labels[b][:, ts_, :], -2.0, part, MULT, ADD)
            for ts_ in (slice(0, 2), slice(2, 4)):
                nc.vector.scalar_tensor_tensor(planes[:, ts_, :], prob[b][:, ts_, :], 1.0, half_sc[b][:, ts_, :], ADD, MULT)
            interleave(True, h[b], planes)
            quantize(hr[b], h[b][:], E5M2)

        def turn_weights(on_vector, b, two_banks):
            words = h_planes[b][:].bitcast(F32).rearrange("p (t q u) -> p t u q", t=PACK, u=2)
            for j, bank in enumerate(two_banks):
                transposes(bank, lambda a: words[:, 2 * j + a // 2, a % 2, :])
                dst = h_turned[:].rearrange("q (b p j a) -> q b j p a", b=B, j=2, a=PACK)[:, b, j]
                copy(on_vector, dst, bank[:].rearrange("q a p -> q p a"))

        def gradient(o, b, t, bank, on_vector):
            product(bank, (xr, wi)[o], block(B * t + b), (hr, hi)[o][b], E5M2)
            copy(on_vector, stages[o][t][:, b * K : (b + 1) * K], flat(bank))

        late_windows = [None] * PACK

        def scatter(on_vector, o, t, first, count):
            out, lst = ((out_0, tail_list), (out_1, head_list))[o]
            window = (windows, late_windows)[o][t]
            dst, src = window[:].indirect(entries(lst, first, count)), stages[o][t][:, first : first + count]
            if on_vector:
                nc.vector.tensor_copy(dst, src)
            else:
                nc.scalar.activation(dst, src, COPY)
            if first + count == LISTED:
                nc.sync.dma_start(out.rearrange("(p t) c -> p t c", t=PACK)[:, t, :], window[:])

        def zeroed_window(t, kib):
            late_windows[t] = placed("late_window%d" % t, [P, T], kib)
            nc.gpsimd.memset(late_windows[t][:], 0.0)

        scores(0, banks[0:4])
        squash(0, banks[4:8])
        quantize(wq[1], w[1][:], E4M3)
        weights(0)
        scores(1, banks[4:8])
        squash(1, banks[0:4])
        turn_weights(False, 0, banks[4:6])
        gradient(0, 0, 2, banks[6], False)
        scatter(False, 0, 2, 0, 256)
        gradient(0, 0, 3, banks[7], False)
        scatter(False, 0, 3, 0, 256)
        scatter(False, 0, 2, 256, 256)
        weights(1)
        quantize(wi, w_turned[:].bitcast(BF16), E4M3)
        turn_weights(True, 1, banks[4:6])
        quantize(wq_both, h_turned[:].bitcast(BF16), E5M2)
        zeroed_window(0, 113)
        zeroed_window(2, 121)
        gradient(0, 1, 0, banks[2], True)
        gradient(0, 0, 0, banks[1], False)
        gradient(0, 1, 2, banks[0], False)
        scatter(True, 0, 0, 0, LISTED)
        zeroed_window(1, 2)
        scatter(False, 0, 2, 512, 256)
        scatter(False, 0, 3, 256, 256)
        scatter(False, 0, 2, 768, 256)
        zeroed_window(3, 24)
        gradient(0, 0, 1, banks[3], False)
        gradient(0, 1, 1, banks[6], False)
        gradient(0, 1, 3, banks[7], False)
        scatter(True, 0, 1, 0, LISTED)
        scatter(False, 0, 3, 512, 256)
        gradient(1, 0, 0, banks[4], False)
        scatter(False, 0, 3, 768, 256)
        gradient(1, 1, 0, banks[5], True)
        gradient(1, 0, 2, banks[0], False)
        gradient(1, 1, 2, banks[1], False)
        scatter(True, 1, 0, 0, LISTED)
        scatter(False, 1, 2, 0, 384)
        gradient(1, 0, 3, banks[2], False)
        scatter(False, 1, 2, 384, 384)
        gradient(1, 1, 3, banks[3], False)
        scatter(False, 1, 2, 768, 256)
        gradient(1, 0, 1, banks[6], True)
        gradient(1, 1, 1, banks[7], True)
        scatter(False, 1, 3, 0, 384)
        scatter(False, 1, 3, 384, 384)
        scatter(False, 1, 3, 768, 256)
        scatter(True, 1, 1, 0, LISTED)
